import numpy as np, ml_dtypes
CORES = [10,34,74,98]
N = 4
import mx_ref
BF = ml_dtypes.bfloat16
def gcols(t, e):
    v = np.concatenate([t.reshape(8, 16, -1, 4), np.zeros((8, 16, 1, 4), BF)], axis=2)
    return np.ascontiguousarray(np.stack([v[g][:, e[g]] for g in range(8)])).reshape(128, -1)
def gpick(z, e):
    return np.concatenate([z[16 * g:16 * g + 16][:, e[g]] for g in range(8)])
def tile(rs):
    return np.stack(rs, axis=2).reshape(128, -1).astype(BF)
def pick(q, e):
    c = np.concatenate([q[0].reshape(128, -1, 4), np.zeros((128, 1, 4), np.uint8)], axis=1); s = np.concatenate([q[1], np.ones((16, 1), np.uint8)], axis=1)
    return (np.ascontiguousarray(c[:, e].reshape(128, -1)), np.ascontiguousarray(s[:, e]))
def join(*qs):
    return (np.concatenate([q[0] for q in qs], axis=1), np.concatenate([q[1] for q in qs], axis=1))
def put(q, e, v):
    c, s = q[0].reshape(128, -1, 4).copy(), q[1].copy(); c[:, e] = v[0].reshape(128, -1, 4); s[:, e] = v[1]
    return (c.reshape(128, -1), s)
def pk(c, s):
    return (np.ascontiguousarray(c), mx_ref.live(s))
def emit(q):
    return q[0], q[1]
def packed(v, rng):
    q = [mx_ref.quantize(np.ascontiguousarray(v[r])) for r in range(N)]
    return np.stack([a for a, b in q]), np.stack([mx_ref.plane(b, rng) for a, b in q])
def values_of_codes():
    e, c = np.zeros((128, 128, 4), np.float32), np.zeros((128, 2, 4), np.uint8)
    e[np.arange(128), np.arange(128), 0] = 1
    c[:127, :, 0] = np.arange(256).reshape(2, 128).T[:127]
    return mx_ref.matmul(mx_ref.quantize(e.reshape(128, 512).astype(BF)), (c.reshape(128, 8), np.full((16, 2), 127, np.uint8))).T.reshape(-1).astype(np.float64)
CODE_VALUE, SCALE_VALUE = values_of_codes(), 2.0 ** (np.arange(256) - 127.0)
def decode(q):
    return (CODE_VALUE[q[0]].reshape(16, 8, -1, 4) * SCALE_VALUE[q[1]][:, None, :, None] + 0.0).reshape(128, -1).astype(np.float32)
def f(rng, *shape):
    return mx_ref.flush((rng.standard_normal(shape, dtype=np.float32) * np.exp2(rng.integers(-2, 3, shape[:-1] + (1,)))).astype(BF))
def wide(rng, *shape, cols=0):
    v = rng.standard_normal(shape, dtype=np.float32) * np.exp2(rng.integers(-12, 13, shape)).astype(np.float32)
    if cols: v *= np.repeat(np.exp2(rng.integers(-cols, cols + 1, shape[:-2] + (1, shape[-1] // 4))) * (rng.random(shape[:-2] + (1, shape[-1] // 4)) > 0.0625), 4, axis=-1).astype(np.float32)
    return mx_ref.flush(v.astype(BF))
C, R = 384, 3
PARTNER = [1, 2, 1]
def fork(m, p):
    base = m + np.maximum(-p[1::16], np.float32(0.0))
    s = p[::16]
    cost = np.stack([base + np.maximum(-s, np.float32(0.0)), base + np.maximum(s, np.float32(0.0))], axis=2).reshape(8, 2 * C) + np.float32(0.0)
    k = np.sort(np.argsort(cost, axis=1, kind="stable")[:, :C], axis=1)
    return k, np.take_along_axis(cost, k, axis=1)
def big(v, k):
    v = v.astype(np.float32) * np.float32(k)
    v[np.abs(v) < np.float32(2.0 ** -16)] = 0
    return v.astype(BF)
def weights(rng, k, still=slice(0)):
    w = big(f(rng, N, 128, 2048), k).reshape(N, 128, 4, 8, 16, 4)
    w[:, :, :, :, still] = 0
    c, p = packed(w.reshape(N, 128, 2048), rng)
    return {"wc": c, "ws": p}
def numbers_of(rng):
    return {"x": big(f(rng, N, 128, 4 * C), 1), "u": np.array(f(rng, N, 128, 512)), "v": np.array(f(rng, N, 128, 512))}
def planted(rng, unit, d, s):
    o = numbers_of(rng)
    x = o["x"].astype(np.float32).reshape(N, 8, 16, C, 4)
    digits = ((d[..., None] >> np.arange(8)) & 1) * 2.0 ** np.arange(8) * unit
    x[:, :, 0] = 0
    x[:, :, 0, :, 0] = -1
    x[:, :, 8] = digits[..., :4]
    x[:, :, 9] = digits[..., 4:]
    x[:, :, 10] = 0
    x[:, :, 10, :, 0] = s
    x[:, :, 11:] = rng.integers(4, 8, (N, 8, 5, C, 4)) * rng.choice([-1.0, 1.0], (N, 8, 5, C, 4)) * (8 * unit)
    u = o["u"].reshape(N, 128, 128, 4)
    u[:, :, ::16] = 0
    u[:, :, 1::16] = 0
    for h in range(0, 128, 16):
        u[:, h + 10, h, 0] = 1
        u[:, h, h + 1, 0] = 1
        u[:, h + 8:h + 10, h + 1] = -1
    return {"x": x.reshape(N, 128, 4 * C).astype(BF), "u": u.reshape(N, 128, 512), "v": o["v"], **weights(rng, 0.25, [0] + [8 + i for i in range(8)])}
def setup_inputs(rng):
    return {**numbers_of(rng), **weights(rng, 1)}
def setup_inputs_ties(rng):
    d = numbers_of(rng)
    e = rng.permutation(N)
    x = d["x"].reshape(N, 8, 16, C, 4)
    for r in range(N):
        k = np.asarray([0, 0, 1, 1, 1, 1, 2])[rng.permutation(C) % 7]
        a = x[r][:, :8, :3].copy()
        a[:, :, 2] = 0
        if r == e[0]: a[:] = 0
        x[r][:, :8] = a[:, :, k]
    x[e[1]] = 0
    u = d["u"].reshape(N, 8, 16, 128, 4)
    u[:, :, 8:, ::16] = 0
    u[:, :, 8:, 1::16] = 0
    g, j = rng.integers(8), rng.integers(C >> R)
    u[e[0], g, :8, 16 * g] = u[e[0], g, :8, 16 * g + 1]
    x[e[0], g, :8, j] = big(u[e[0], g, :8, 16 * g], 1)
    return {"x": x.reshape(N, 128, 4 * C), "u": u.reshape(N, 128, 512), "v": d["v"], **weights(rng, 1, slice(8))}
def setup_inputs_near(rng):
    d = np.argsort(rng.random((N, 8, C)), axis=2) // 2
    q = np.stack([rng.permutation(8) for r in range(N)])
    d[q % 4 == 0] = (np.arange(C) // 2 + C // 4 + 1) % (C // 2)
    o = planted(rng, 2.0 ** -23, d, rng.choice([-1.0, 1.0], (N, 8, C)) * 2.0 ** -23)
    x = o["x"].reshape(N, 8, 16, C, 4)
    for r in range(N):
        for g in range(8):
            if q[r, g] % 2: x[r, g, 0, np.argmax(d[r, g]), 0] = -2.0 ** 30
            if q[r, g] % 4 == 0:
                j = np.argmin(d[r, g])
                x[r, g, :8, j] = 0
                x[r, g, 0, j, 0] = -2.0 ** -24
    return {**o, "x": x.reshape(N, 128, 4 * C)}
def setup_inputs_ends(rng):
    once = np.stack([rng.permutation(8) % 2 for r in range(N)])[:, :, None] == 1
    d = np.where(once, rng.integers(0, 16, (N, 8, C)), (C - 1 - np.arange(C)) // 2)
    s = np.where(once, 4.0, 2.0 ** -9) * rng.choice([-1.0, 1.0], (N, 8, C))
    return planted(rng, 2.0 ** -6, d, s)
def setup_inputs_huge(rng):
    d = numbers_of(rng)
    low = np.where(rng.permutation(N) < N // 2, 0.25, 0.45)[:, None]
    c = low + (0.7 - low) * rng.random((N, C))
    x = 2.0 ** 30 * c[:, None, :, None] * (0.9 + 0.1 * rng.random((N, 128, C, 4)))
    u = d["u"].reshape(N, 128, 128, 4)
    a = 2.0 ** 30 * (1 - 0.25 * rng.random((2, N, 128, 8, 4)))
    u[:, :, ::16] = (a[0] * rng.choice([-1.0, 1.0], a[0].shape)).astype(np.float32).astype(BF)
    u[:, :, 1::16] = (-a[1]).astype(np.float32).astype(BF)
    return {"x": x.astype(np.float32).reshape(N, 128, 4 * C).astype(BF), "u": u.reshape(N, 128, 512), "v": d["v"], **weights(rng, 2.0 ** -8)}
def setup_inputs_spread(rng):
    d = setup_inputs(rng)
    d["x"] = big(wide(rng, N, 128, 4 * C, cols=6), 1)
    return d
def check_inputs(d):
    b = []
    for k in ("x", "u", "v"):
        a = np.abs(d[k].astype(np.float32))
        if not (np.isfinite(a).all() and ((a == 0) | (a >= 2.0 ** -30) & (a <= 2.0 ** 30)).all()): b.append("a value of " + k)
    return b
def reference(x, u, v, wc, ws):
    qu = [mx_ref.quantize(u[r]) for r in range(N)]
    lay = [[pick(pk(wc[r], ws[r]), np.arange(128 * b, 128 * b + 128)) for b in range(4)] for r in range(N)]
    now = [x[r] for r in range(N)]
    m = np.zeros((N, 8, C), np.float32)
    for t in range(R):
        k, z, sent = [], [], []
        for r in range(N):
            q = mx_ref.quantize(now[r])
            e, m[r] = fork(m[r], mx_ref.matmul(qu[r], q))
            k.append(e)
            z.append(gcols(decode(q).astype(BF), e // 2))
            sent.append(mx_ref.quantize(z[r]))
        for r in range(N):
            sign = np.repeat(1 - 2 * (k[r] % 2), 16, axis=0).astype(np.float32)
            h = [gpick(mx_ref.matmul(lay[r][b], sent[r ^ PARTNER[t]]) * np.float32(0.015625), k[r] // 2) for b in range(4)]
            a = z[r].astype(np.float32).reshape(128, C, 4)
            now[r] = tile([a[:, :, b] + sign * h[b] for b in range(4)])
    y, kl = np.zeros((N, 128, C), np.float32), np.zeros((N, 8, C), np.float32)
    oc, osc = np.zeros((N, 128, 4 * C), np.uint8), np.zeros((N, 16, C), np.uint8)
    for r in range(N):
        q = mx_ref.quantize(now[r])
        y[r] = mx_ref.matmul(mx_ref.quantize(v[r]), q)
        kl[r] = k[r]
        oc[r], osc[r] = emit(q)
    return {"y": y, "kl": kl, "ml": m, "oc": oc, "osc": osc}

@@ -1,0 +1,454 @@
+from concourse.mybir import dt, AluOpType, AxisListType, ActivationFunctionType
+
+Op, Fn = AluOpType, ActivationFunctionType
+C, R = 384, 3
+H = C // 2
+PARTNER = [1, 2, 1]
+UP = 2.0 ** 20
+NIL = 2.0 ** -100
+NA = {1: 576, 2: 512, 3: 512, 4: 464, 5: 464, 6: 464, 8: 496}
+EMPTY, HOLD = 512, 4096.0
+SLOTS = 2 * C + 2
+DUMP = 2 * C + 8
+WIN = DUMP + 128 * 24 + 2 * C
+F32, BF, U16, I32, Q, U8 = "float32", "bfloat16", "uint16", "int32", "float8_e4m3fn_x4", "uint8"
+
+
+def sb(n, d):
+    return ("sbuf", [128, n], d)
+
+
+SCRATCH = {
+    "xt": sb(4 * C, BF), "tt": sb(4 * C, BF), "zt": sb(4 * C, BF), "ut": sb(512, BF), "vt": sb(512, BF),
+    "qu": sb(128, Q), "su": sb(128, U8), "qp": sb(256, Q), "sp": sb(256, U8), "qv": sb(128, Q), "sv": sb(128, U8),
+    "qw": sb(512, Q), "sw": sb(512, U8), "qz": sb(C, Q), "sz": sb(C, U8), "qe": sb(1024, Q), "se": sb(1024, U8),
+    "ep": sb(516, BF), "en": sb(516, BF),
+    "ip": sb(1, I32), "ip2": sb(1, I32), "iu": sb(16, I32), "ou": sb(16, U16), "i49": sb(49, F32),
+    "col": sb(32, F32), "lo2": sb(2, BF), "oh": sb(16, F32), "tri": sb(16, F32), "c64": sb(17, F32), "c2": sb(17, F32),
+    "g12": sb(17, F32), "g2": sb(17, F32), "tmp": sb(32, F32), "t1": sb(18, F32), "t2": sb(18, F32), "wm": sb(18, F32),
+    "ctab": sb(48, F32), "wn": sb(48, F32), "off": sb(2, U16), "gat": sb(32, F32), "gat2": sb(32, F32),
+    "xx": sb(2 * C, F32), "yy": sb(2 * C, F32), "rr": sb(2 * C, F32), "nz": sb(C, F32), "ab": sb(C, F32),
+    "sg": sb(C, F32), "mm": sb(C, F32), "rg": sb(C, F32), "junk": sb(2 * C, BF), "fl": sb(304, BF), "sc": sb(152, BF),
+    "bd": sb(24, F32), "sd": sb(24, F32), "rd": sb(48, F32), "xd": sb(48, F32), "yd": sb(48, F32), "ye": sb(24, F32),
+    "ae": sb(100, F32), "keep": sb(100, F32), "pp": sb(100, F32), "o2": sb(2, U16), "tab": sb(3 * 784, BF),
+    "w1": sb(24, F32), "w2": sb(24, F32), "za": sb(24, F32), "h0": sb(96, F32), "h1": sb(96, F32), "hs": sb(96, F32),
+    "osl": sb(24, U16), "val": sb(C, BF), "win": sb(WIN, BF), "i16": sb(400, BF), "dk": sb(800, BF),
+    "sk": sb(SLOTS, "float16"), "mk": sb(24, F32), "ok": sb(24, U16),
+    "dd": sb(4 * C, BF), "ff": sb(8 * C, BF), "i768": sb(2 * C, F32), "kr": sb(C, F32), "mr": sb(C, F32),
+    "ya": sb(H, F32), "yb": sb(H, F32),
+}
+for _t in range(R + 1):
+    SCRATCH["qt%d" % _t] = sb(C, Q)
+    SCRATCH["st%d" % _t] = sb(C, U8)
+for _t in range(R):
+    SCRATCH["lq%d" % _t] = sb(C, Q)
+    SCRATCH["ls%d" % _t] = sb(C, U8)
+    SCRATCH["oa%d" % _t] = sb(24, U16)
+    SCRATCH["la%d" % _t] = sb(24, U16)
+for _b in range(8):
+    SCRATCH["ps%d" % _b] = ("psum", [128, 512], F32)
+
+POOL = {"v": 36, "a": 36, "p": 20, "g": 20, "d": 24}
+SEMAPHORES = ["%s%d" % (k, i) for k in POOL for i in range(POOL[k])]
+SEMAPHORES += ["%s%d" % (k, t) for k in ("aq", "al", "sq", "sl") for t in range(R)]
+
+
+def emit(g, T, ops):
+    eng = {"v": g.vector, "a": g.scalar, "p": g.tensor, "g": g, "s": g.sync}
+    writer, readers, known, after, waits, needed = {}, {}, {k: 0 for k in eng}, {}, [], set()
+    group = {}
+    for i, o in enumerate(ops):
+        group.setdefault(o["grp"] or i, []).append(i)
+    end = [group[o["grp"] or i][-1] for i, o in enumerate(ops)]
+    for i, o in enumerate(ops):
+        q = o["q"]
+        deps = set(o["also"])
+        for t in o["r"]:
+            if t in writer:
+                deps.add(writer[t])
+            if t.startswith("ps"):
+                deps.update(j for j in readers.get(t, []) if ops[j]["q"] != q)
+        for t in o["w"]:
+            if t in writer and not (q == "p" and ops[writer[t]]["q"] == "p"):
+                deps.add(writer[t])
+            deps.update(readers.get(t, []))
+        mine = []
+        deps = set(end[j] for j in deps)
+        if q in eng:
+            for j in sorted(deps, reverse=True):
+                if not known[q] >> j & 1:
+                    mine.append(j)
+                    known[q] |= after[j]
+            needed.update(mine)
+            after[i] = known[q] | sum(1 << j for j in group[o["grp"] or i] if j <= i)
+        else:
+            after[i] = 1 << i
+        waits.append((mine, known.get(q, 0)))
+        for t in o["r"]:
+            readers.setdefault(t, []).append(i)
+        for t in o["w"]:
+            writer[t] = i
+            readers[t] = []
+    last, count, mark, taken = {}, {}, {}, {}
+    for i, o in enumerate(ops):
+        q = o["q"]
+        if o["sem"] is not None:
+            mark[i] = o["sem"]
+        if q not in eng:
+            continue
+        mine, kn = waits[i]
+        for j in mine:
+            eng[q].wait_ge(T.sem[mark[j][0]], mark[j][1])
+        if o["f"] is None:
+            continue
+        ins = o["f"](eng[q])
+        if o["sem"] is None and end[i] in needed:
+            pool, step = ("d", 16) if o["dma"] else (q, 1)
+            if end[i] not in taken:
+                free = [n for n in ("%s%d" % (pool, k) for k in range(POOL[pool])) if n not in last or kn >> last[n] & 1]
+                taken[end[i]] = free[0]
+            name = taken[end[i]]
+            last[name] = end[i]
+            count[name] = count.get(name, 0) + step
+            ins.then_inc(T.sem[name], step)
+            mark[i] = (name, count[name])
+
+
+def rank_program(g, core, T, topo):
+    rank = T.rank_of(core)
+    if rank is None:
+        return
+    ops, must, together = [], [], [None]
+
+    def joint(name):
+        together[0] = name
+
+    def add(q, f, r, w, sem=None, dma=False, also=()):
+        ops.append({"q": q, "f": f, "r": r.split(), "w": w.split(), "sem": sem, "dma": dma, "also": list(also),
+                    "grp": together[0] and together[0] + q})
+        return len(ops) - 1
+
+    def dma(q, out, in_, r, w):
+        return add(q, lambda e: e.dma_start(out, in_), r, w, dma=True)
+
+    def ts(out, in0, s1, o0, r, w, s2=None, o1=None):
+        if o1 is None:
+            return add("v", lambda e: e.tensor_scalar(out, in0, s1, None, o0), r, w)
+        return add("v", lambda e: e.tensor_scalar(out, in0, s1, s2, o0, o1), r, w)
+
+    def tt(out, a, b, op, r, w):
+        return add("v", lambda e: e.tensor_tensor(out, a, b, op), r, w)
+
+    def cp(out, in_, r, w):
+        return add("v", lambda e: e.tensor_copy(out, in_), r, w)
+
+    def scan(out, d0, d1, init, o0, o1, r, w):
+        return add("v", lambda e: e.tensor_tensor_scan(out, d0, d1, init, o0, o1), r, w)
+
+    def red(out, in_, op, r, w):
+        return add("v", lambda e: e.tensor_reduce(out, in_, AxisListType.X, op), r, w)
+
+    def fill(ap, c, w):
+        return add("v", lambda e: e.memset(ap, c), "", w)
+
+    def quant(out, sc, in_, r, w):
+        return add("v", lambda e: e.quantize_mx(out, sc, in_), r, w)
+
+    def act(out, in_, fn, r, w, bias=0.0, scale=1.0, acc=None):
+        if acc is None:
+            return add("a", lambda e: e.activation(out, in_, fn, bias=bias, scale=scale), r, w)
+        return add("a", lambda e: e.activation(out, in_, fn, bias=bias, scale=scale, accum_out=acc), r, w)
+
+    def acopy(out, in_, r, w):
+        return add("a", lambda e: e.activation(out, in_, Fn.Copy), r, w)
+
+    def iota(out, pat, base, cm, w, small=True):
+        if small:
+            return add("g", lambda e: e.iota(out, pat, base, cm, allow_small_or_imprecise_dtypes=True), "", w)
+        return add("g", lambda e: e.iota(out, pat, base, cm), "", w)
+
+    def mx(bank, n, lq, ls, rq, rs, start, stop, r):
+        return add("p", lambda e: e.matmul_mx(T["ps%d" % bank][:, 0:n], lq, ls, rq, rs, start, stop), r, "ps%d" % bank)
+
+    def send(pairs, dst, arrive, left, r):
+        rid, pid = topo.addr(dst)[:2]
+        mask = topo.mask(core, dst)
+        n = len(topo.engines(core, dst)) * len(pairs)
+
+        def f(e):
+            for out, in_ in pairs:
+                e.remote_dma(out, in_, T.sem[arrive], T.sem[left], pid, rid, mask)
+        must.append(add("g", f, r, "", sem=(left, n)))
+
+    def arrival(src, name, writes, w):
+        must.append(add("x", None, "", w, sem=(name, len(topo.engines(src, core)) * writes)))
+
+    names = ["pm", "pm1", "pw", "f", "ipw", "rc", "f2", "th1", "th2", "th3", "th7", "thy", "ts", "nacc", "beta", "gam"]
+    col = {n: T.col[:, i:i + 1] for i, n in enumerate(names)}
+    u8 = dt.uint8
+
+    dma("a", T.ut[:], T.u[:], "", "ut")
+    dma("s", T.xt[:, 0:4 * H], T.x[:, 0:4 * H], "", "xta")
+    dma("s", T.xt[:, 4 * H:4 * C], T.x[:, 4 * H:4 * C], "", "xtb")
+    add("s", None, "xta xtb", "")
+    dma("s", T.qw[:].bitcast(u8), T.wc[:], "", "qw")
+    dma("s", T.sw[:], T.ws[:], "", "sw")
+    dma("s", T.vt[:], T.v[:], "", "vt")
+    iota(T.ip[:], [[0, 1]], 0, 1, "ip", small=False)
+    iota(T.iu[:], [[1, 2], [16, 8]], 0, 0, "iu", small=False)
+    iota(T.i49[:], [[1, 49]], 0, 0, "i49")
+    fill(T.ep[:], 64.0, "ep")
+    fill(T.en[:], -64.0, "en")
+    fill(T.c64[:], 64.0, "c64")
+    fill(T.c2[:], 2.0, "c2")
+    for n in ("ep", "en"):
+        if n == "en":
+            iota(T.i16[:], [[0, 25], [1, 16]], 0, 0, "i16")
+        add("g", lambda e, n=n: e.affine_select(T[n][:], T[n][:], [[1, 516]], Op.is_equal, 0.0, -3, -4), n, n)
+    ts(T.ip2[:], T.ip[:], 15, Op.bitwise_and, "ip", "ip2")
+    cp(T.ou[:], T.iu[:], "iu", "ou")
+    scan(T.g12[:], T.c64[:], T.c64[:], NIL / 4096.0, Op.mult, Op.mult, "c64", "g12")
+    cp(col["pm"], T.ip2[:], "ip2", "pm")
+    scan(T.g2[:], T.c2[:], T.c2[:], 1.0, Op.mult, Op.max, "c2", "g2")
+    ts(T.oh[:], T.i49[:, 0:16], col["pm"], Op.is_equal, "i49 pm", "oh")
+    ts(T.tri[:], T.i49[:, 0:16], col["pm"], Op.is_lt, "i49 pm", "tri")
+    ts(T.off[:, 1:2], col["pm"], 2.0, Op.add, "pm", "off1", 4.0, Op.min)
+    tt(T.tmp[:, 0:16], T.g12[:, 1:17], T.oh[:], Op.mult, "g12 oh", "tmpa")
+    tt(T.tmp[:, 16:32], T.g2[:, 0:16], T.oh[:], Op.mult, "g2 oh", "tmpb")
+    act(col["pm1"], col["pm"], Fn.Identity, "pm", "pm1", bias=1.0)
+    act(col["f"], col["pm"], Fn.Identity, "pm", "f", bias=17.0 / 16, scale=1.0 / 16)
+    act(col["f2"], col["pm"], Fn.Identity, "pm", "f2", bias=17.0 / 32, scale=1.0 / 32)
+    red(col["th1"], T.tmp[:, 0:16], Op.add, "tmpa", "th1")
+    red(col["pw"], T.tmp[:, 16:32], Op.add, "tmpb", "pw")
+    add("v", lambda e: e.reciprocal(T.col[:, 4:6], T.col[:, 2:4]), "pw f", "ipw rc")
+    ts(T.t1[:, 1:17], T.g12[:, 1:17], col["pw"], Op.mult, "g12 pw", "t1")
+    act(T.t1[:, 0:1], col["pm"], Fn.Identity, "pm", "t1a", scale=0.0)
+    act(T.t1[:, 17:18], col["pw"], Fn.Identity, "pw", "t1b", scale=NIL / 16)
+    act(T.t2[:, 0:1], col["pm"], Fn.Identity, "pm", "t2a", scale=0.0)
+    act(T.t2[:, 17:18], col["f"], Fn.Identity, "f", "t2b", scale=1.0 / 16)
+    ts(T.t2[:, 1:17], T.g2[:, 0:16], col["f2"], Op.mult, "g2 f2", "t2")
+    act(T.ctab[:], T.i49[:, 0:48], Fn.Identity, "i49", "ctab0", scale=0.0)
+    steps = [2.0 ** -4, 2.0 ** -8, 2.0 ** -12, 2.0 ** -16, 2.0 ** -20, 2.0 ** -23]
+    cells = [(8 * k + 1, 0.0, steps[k]) for k in range(6)]
+    cells += [(8 * k + 3, steps[k + 1] - steps[k], steps[k + 1] - steps[k]) for k in range(4)]
+    cells += [(2, 1.0 / 16, 17.0 / 16), (35, steps[5] - steps[4], steps[5] / 2 - steps[4]), (45, steps[5], steps[5] / 2)]
+    joint("cells")
+    for c, a, b in cells:
+        act(T.ctab[:, c:c + 1], col["pm"], Fn.Identity, "pm ctab0", "ctab%d" % (c + 1), bias=b, scale=a)
+    joint(None)
+    ctab = " ".join("ctab%d" % (c + 1) for c, a, b in cells)
+
+    def late_g():
+        iota(T.ae[:], [[0, 100]], 0, 0, "ae0")
+        iota(T.keep[:], [[0, 100]], 1, 0, "keep")
+        iota(T.keep[:, 50:51], [[0, 1]], 0, 0, "keep")
+        iota(T.tab[:, 0:784], [[0, 16], [1, 49]], 0, 0, "tab0")
+        iota(T.h0[:], [[0, 96]], 1, 0, "h0")
+        iota(T.h0[:, 0:96:4], [[0, 24]], 0, 0, "h0")
+        iota(T.h0[:, 1:96:4], [[1, 24]], DUMP, 24, "h0")
+        iota(T.val[:], [[1, 24], [24, 16]], -H, 0, "val")
+        iota(T.win[:, 0:SLOTS], [[0, SLOTS]], EMPTY, 0, "win")
+
+    def tri_a(lo, hi):
+        joint("tri")
+        for i in range(lo, hi):
+            act(T.tab[:, 784 + 49 * i:833 + 49 * i], T.i49[:], Fn.Identity, "i49 tri", "tab1_%d" % i, scale=T.tri[:, i:i + 1])
+        joint(None)
+    tab1 = " ".join("tab1_%d" % i for i in range(16))
+
+    def qe(k):
+        src, b = ("ep", "en")[k // 4], k % 4
+        quant(T.qe[:, 128 * k:128 * k + 128], T.se[:, 128 * k:128 * k + 128], T[src][:, 3 - b:515 - b], src, "qe%d" % k)
+
+    def hold(out, c, w):
+        ts(out, T.i16[:], col["pm"], Op.is_equal, "i16 pm", w, c, Op.mult)
+
+    def halves(k, tile, ra, rb):
+        quant(T["qt%d" % k][:, 0:H], T["st%d" % k][:, 0:H], tile[:, 0:4 * H], ra, "qt%da" % k)
+        quant(T["qt%d" % k][:, H:C], T["st%d" % k][:, H:C], tile[:, 4 * H:4 * C], rb, "qt%db" % k)
+
+    qe(0)
+    qe(1)
+    quant(T.qu[:], T.su[:], T.ut[:], "ut", "qu")
+    acopy(T.sp[:], T.su[:].indirect(T.ou[:]), "qu ou", "sp")
+    cp(T.qp[:].bitcast(dt.uint32), T.qu[:].bitcast(dt.uint32).indirect(T.ou[:]), "qu ou", "qp")
+    tri_a(0, 14)
+    halves(0, T.xt, "xta", "xtb")
+
+    def rest_a():
+        tri_a(14, 16)
+        dma("s", T.tab[:, 1568:2352], T.tab[:, 784:1568], tab1, "tab2")
+
+    def ends_a():
+        act(T.ae[:, 49:50], col["pm"], Fn.Identity, "pm ae0", "ae49", scale=49.0)
+        act(T.ae[:, 99:100], col["pm"], Fn.Identity, "pm ae0", "ae99", scale=49.0, bias=784.0)
+
+    idle_v = {(0, 1): lambda: hold(T.dk[:, 0:800:2], HOLD, "dk0"), (0, 2): lambda: hold(T.dk[:, 1:800:2], 0.5, "dk1"),
+              (0, 3): lambda: qe(2), (0, 4): lambda: qe(3), (0, 5): lambda: qe(4),
+              (1, 3): lambda: quant(T.qv[:], T.sv[:], T.vt[:], "vt", "qv")}
+    idle_a = {(0, 1): rest_a, (0, 3): ends_a}
+
+    for t in range(R):
+        mate = T.cores[rank ^ PARTNER[t]]
+        qt, st, lq, ls, oa, la = (T["%s%d" % (n, t)] for n in ("qt", "st", "lq", "ls", "oa", "la"))
+        tq = "qt%da qt%db" % (t, t)
+        mx(0, H, T.qp[:, 128:256], T.sp[:, 128:256], qt[:, 0:H], st[:, 0:H], True, True, "qp sp qt%da" % t)
+        mx(2, H, T.qp[:, 128:256], T.sp[:, 128:256], qt[:, H:C], st[:, H:C], True, True, "qp sp qt%db" % t)
+        mx(1, C, T.qp[:, 0:128], T.sp[:, 0:128], qt[:], st[:], True, True, "qp sp " + tq)
+        send([(lq[:].bitcast(u8), qt[:].bitcast(u8)), (ls[:], st[:])], mate, "aq%d" % t, "sq%d" % t, tq)
+        arrival(mate, "aq%d" % t, 2, "lq%d" % t)
+        if t == 0:
+            late_g()
+        if t == 1:
+            iota(T.i768[:], [[1, 2 * C]], 0, 0, "i768")
+        for a, bank, n in ((0, 0, "a"), (H, 2, "b")):
+            z = T["ps%d" % bank][:, 0:H]
+            if t == 0:
+                ts(T.xx[:, a:a + H], z, -UP, Op.mult, "ps%d" % bank, "xb" + n, NIL, Op.max)
+            else:
+                act(T.nz[:, a:a + H], z, Fn.Relu, "ps%d" % bank, "nz" + n, scale=-UP)
+                tt(T.xx[:, a:a + H], T.mm[:, a:a + H], T.nz[:, a:a + H], Op.add, "mm nz" + n, "xb" + n)
+        act(T.ab[:], T.ps1[:, 0:C], Fn.Abs, "ps1", "ab", scale=UP)
+        tt(T.xx[:, C:C + H], T.xx[:, 0:H], T.ab[:, 0:H], Op.add, "xba ab", "xc")
+        tt(T.xx[:, C + H:2 * C], T.xx[:, H:C], T.ab[:, H:C], Op.add, "xbb ab", "xe")
+        act(T.sg[:], T.ps1[:, 0:C], Fn.Copy, "ps1", "sg", scale=UP)
+        dma("s", T.bd[:], T.xx[0:128:16, 0:C], "xba xbb", "bd")
+        dma("s", T.sd[:], T.sg[0:128:16, :], "sg", "sd")
+        idle_a[t, 5] = lambda: (act(T.rd[:, 0:48:2], T.sd[:], Fn.Relu, "sd", "rd0", scale=-1.0),
+                                act(T.rd[:, 1:48:2], T.sd[:], Fn.Relu, "sd", "rd1"))
+
+        def count(k, data, tok_a, tok_v, th, tth, between=None, behind=None):
+            na = NA[k]
+            act(T.junk[:, 0:na], data[:, 0:na], Fn.Sign, tok_a + " " + tth, "nacc junk", bias=th, scale=-1.0, acc=col["nacc"])
+            idle_a.get((t, k), lambda: 0)()
+            nv = 2 * C - na
+            ts(T.fl[:, 0:nv], data[:, na:2 * C], th, Op.is_gt, tok_v + " " + tth, "fl", 2.0, Op.mult)
+            if between:
+                between()
+            scan(T.sc[:, 0:nv // 2], T.fl[:, 0:nv // 2], T.fl[:, nv // 2:nv], -float(nv), Op.add, Op.add, "fl", "sc")
+            if behind:
+                behind()
+            last = T.sc[:, nv // 2 - 1:nv // 2]
+            if k <= 2:
+                ts(T.off[:, 0:1], last, col["nacc"], Op.is_gt, "sc nacc pm1", "off0", col["pm1"], Op.mult)
+            else:
+                ts(T.off[:, 0:1], last, col["nacc"], Op.is_gt, "sc nacc", "off0")
+
+        def climb(k, table, r, w):
+            act(T.gat2[:, 0:16], table[:, 0:17].indirect(T.off[:, 0:1]), Fn.Identity, "off0 " + r, "gat2 " + w,
+                bias=table[:, 17:18], acc=col[w])
+            idle_v.get((t, k), lambda: 0)()
+
+        def step(k, out, w):
+            a = 8 * (k - 3)
+            act(T.gat2[:], T.wn[:, a:a + 5].indirect(T.off[:]), Fn.Identity, "off0 off1 wn wn%d" % k, "gat2 " + w, acc=out)
+            idle_v.get((t, k), lambda: 0)()
+
+        count(1, T.xx, "xba xbb xc", "xe", col["th1"], "th1")
+        climb(1, T.t1, "t1 t1a t1b", "th2")
+        count(2, T.xx, "xba xbb xc", "xc xe", col["th2"], "th2",
+              lambda: ts(T.lo2[:, 1:2], col["th2"], col["ipw"], Op.mult, "th2 ipw", "lo1"),
+              lambda: ts(T.wm[:], T.t2[:], T.lo2[:, 1:2], Op.mult, "lo1 t2 t2a t2b", "wm"))
+        climb(2, T.wm, "wm", "th3")
+        count(3, T.xx, "xba xbb xc", "xc xe", col["th3"], "th3",
+              lambda: ts(T.lo2[:, 0:1], col["th3"], col["rc"], Op.mult, "th3 rc", "lo2"),
+              lambda: ts(T.wn[:], T.ctab[:], T.lo2[:, 0:1], Op.mult, "lo2 ctab0 " + ctab, "wn wn3 wn4 wn5 wn6 wn7 wn8"))
+        step(3, T.wn[:, 10:11], "wn4")
+        count(4, T.xx, "xba xbb xc", "xc xe", T.wn[:, 10:11], "wn4")
+        step(4, T.wn[:, 18:19], "wn5")
+        count(5, T.xx, "xba xbb xc", "xc xe", T.wn[:, 18:19], "wn5")
+        step(5, T.wn[:, 26:27], "wn6")
+        count(6, T.xx, "xba xbb xc", "xc xe", T.wn[:, 26:27], "wn6")
+        step(6, col["th7"], "th7")
+        tt(T.xd[:, 0:48:2], T.bd[:], T.rd[:, 0:48:2], Op.add, "bd rd0", "xd0")
+        tt(T.xd[:, 1:48:2], T.bd[:], T.rd[:, 1:48:2], Op.add, "bd rd1", "xd1")
+        act(T.junk[:], T.xx[:], Fn.Sign, "xba xbb xc xe th7", "nacc junk", bias=col["th7"], scale=-1.0, acc=col["nacc"])
+        ts(T.yy[:], T.xx[:], col["th7"], Op.subtract, "xba xbb xc xe th7", "yy")
+        ts(T.off[:, 0:1], col["nacc"], 0.0, Op.is_lt, "nacc", "off0")
+        step(7, col["thy"], "thy")
+        ts(T.yd[:], T.xd[:], col["th7"], Op.subtract, "xd0 xd1 th7", "yd")
+        ts(T.ye[:], T.bd[:], col["th7"], Op.subtract, "bd th7", "ye")
+        count(8, T.yy, "yy", "yy", col["thy"], "thy",
+              lambda: ts(T.wn[:, 42:43], col["thy"], T.wn[:, 45:46], Op.subtract, "thy wn", "wn8"))
+        step(8, col["ts"], "ts")
+
+        for b in range(4):
+            mx(2 + b, C, T.qe[:, 128 * b:128 * b + 128], T.se[:, 128 * b:128 * b + 128], lq[:], ls[:], True, True,
+               "qe%d lq%d" % (b, t))
+
+        ts(T.ae[:, 1:49], T.yd[:], col["ts"], Op.is_lt, "yd ts ae0", "aea")
+        ts(T.ae[:, 51:99], T.yd[:], col["ts"], Op.is_equal, "yd ts ae0", "aee")
+        act(T.w1[:], T.ye[:], Fn.Sign, "ye ts", "w1", bias=col["ts"], scale=-1.0)
+        act(T.w2[:], T.w1[:], Fn.Identity, "w1", "w2", scale=-1024.0)
+        scan(T.pp[:], T.keep[:], T.ae[:], 0.0, Op.mult, Op.add, "keep aea aee ae49 ae99", "pp")
+        cp(T.o2[:], T.pp[:, 49:100:50], "pp", "o2")
+        act(T.gat2[:], T.tab[:, 0:1568].indirect(T.o2[:]), Fn.Identity, "o2 tab0 " + tab1, "gat2 beta",
+            bias=C / 32.0, scale=-1.0, acc=col["beta"])
+        act(T.gat[:], T.tab[:, 784:2352].indirect(T.o2[:]), Fn.Identity, "o2 tab2 " + tab1, "gat gam",
+            bias=-1.0 / 32, scale=2.0, acc=col["gam"])
+        tt(T.za[:], T.pp[:, 50:98:2], T.w2[:], Op.add, "pp w2", "za")
+        tt(T.h1[:, 2:96:4], T.pp[:, 1:49:2], T.pp[:, 2:49:2], Op.add, "pp", "h1c")
+        ts(T.h1[:, 1:96:2], T.pp[:, 51:99], col["beta"], Op.min, "pp beta", "h1b")
+        ts(T.h1[:, 0:96:4], T.za[:], col["beta"], Op.is_ge, "za beta", "h1a")
+        for b in range(4):
+            act(T.dd[:, C * b:C * b + C], T["ps%d" % (2 + b)][:, 0:C], Fn.Copy, "ps%d" % (2 + b), "dd%d" % b, scale=1.0 / 64)
+        act(T.rr[:, 0:2 * C:2], T.sg[:], Fn.Relu, "sg", "r0", scale=-1.0)
+        act(T.rr[:, 1:2 * C:2], T.sg[:], Fn.Relu, "sg", "r1")
+        scan(T.hs[:], T.h0[:], T.h1[:], 0.0, Op.mult, Op.add, "h0 h1a h1b h1c", "hs")
+        ts(T.osl[:], T.hs[:, 3:96:4], col["gam"], Op.add, "hs gam", "osl")
+        cp(T.win[:].indirect(T.osl[:]), T.val[:], "osl val", "win")
+        scan(T.sk[:], T.dk[:, 0:SLOTS], T.win[:, 0:SLOTS], 0.0, Op.add, Op.min, "dk0 dk1 win", "sk")
+        tt(T.mk[:], T.sk[:, 31:2 * C:32], T.sk[:, 32:2 * C + 1:32], Op.min, "sk", "mk")
+        ts(oa[:], T.mk[:], H - 0.25, Op.add, "mk", "oa%d" % t)
+        send([(la[:], oa[:])], mate, "al%d" % t, "sl%d" % t, "oa%d" % t)
+        arrival(mate, "al%d" % t, 1, "la%d" % t)
+
+        ts(T.ok[:], T.mk[:], 2.0, Op.mult, "mk", "ok", float(C), Op.add)
+        acopy(T.rg[:], T.rr[:].indirect(T.ok[:]), "r0 r1 ok", "rg")
+        if t == 0:
+            qe(5)
+            qe(6)
+            qe(7)
+        tt(T.mm[:], T.xx[:, 0:C].indirect(oa[:]), T.rg[:], Op.add, "xba xbb oa%d rg" % t, "mm")
+        if t < R - 1:
+            iota(T.win[:, 0:SLOTS], [[0, SLOTS]], EMPTY, 0, "win")
+        else:
+            acopy(T.kr[:], T.i768[:].indirect(T.ok[:]), "i768 ok", "kr")
+            must.append(dma("s", T.kl[:], T.kr[0:128:16, :], "kr", ""))
+        order = [(0, 0, 6), (2, 0, 7), (0, 1, 0), (2, 1, 1), (1, 0, 2), (3, 0, 3), (1, 1, 4), (3, 1, 5)]
+        for b, s, bank in order:
+            k = 4 * s + b
+            mx(bank, C, T.qe[:, 128 * k:128 * k + 128], T.se[:, 128 * k:128 * k + 128], qt[:], st[:], True, False,
+               "qe%d %s" % (k, tq))
+
+        for b in range(4):
+            (cp, acopy)[b // 2](T.zt[:, b:4 * C:4], T.dd[:, C * b:C * b + C].indirect(la[:]), "dd%d la%d" % (b, t), "zt%d" % b)
+        quant(T.qz[:], T.sz[:], T.zt[:], "zt0 zt1 zt2 zt3", "qz")
+        for b, s, bank in order:
+            mx(bank, C, T.qw[:, 128 * b:128 * b + 128], T.sw[:, 128 * b:128 * b + 128], T.qz[:], T.sz[:], False, True, "qw sw qz")
+        for b, s, bank in order:
+            out, src, c = T.ff[:, 2 * C * b + s:2 * C * (b + 1):2], T["ps%d" % bank][:, 0:C], (1 - 2 * s) / 64.0
+            if b < 2:
+                ts(out, src, c, Op.mult, "ps%d" % bank, "ff%d%d" % (b, s))
+            else:
+                act(out, src, Fn.Copy, "ps%d" % bank, "ff%d%d" % (b, s), scale=c)
+            if b % 2:
+                b -= 1 - s
+                (cp, acopy)[b // 2](T.tt[:, b:4 * C:4], T.ff[:, 2 * C * b:2 * C * (b + 1)].indirect(T.ok[:]),
+                                    "ff%d0 ff%d1 ok" % (b, b), "tt%d" % b)
+        halves(t + 1, T.tt, "tt0 tt1 tt2 tt3", "tt0 tt1 tt2 tt3")
+
+    qt, st, tq = T["qt%d" % R], T["st%d" % R], "qt%da qt%db" % (R, R)
+    act(T.mr[:], T.mm[:], Fn.Identity, "mm", "mr", bias=-NIL / UP, scale=1.0 / UP)
+    must.append(dma("a", T.ml[:], T.mr[0:128:16, :], "mr", ""))
+    for a, bank, n in ((0, 0, "a"), (H, 1, "b")):
+        mx(bank, H, T.qv[:], T.sv[:], qt[:, a:a + H], st[:, a:a + H], True, True, "qv qt%d%s" % (R, n))
+        must.append(dma("s", T.oc[:, 4 * a:4 * a + 4 * H], qt[:, a:a + H].bitcast(u8), "qt%d%s" % (R, n), ""))
+    acopy(T.ya[:], T.ps0[:, 0:H], "ps0", "ya")
+    must.append(dma("a", T.y[:, 0:H], T.ya[:], "ya", ""))
+    cp(T.yb[:], T.ps1[:, 0:H], "ps1", "yb")
+    for k in range(4):
+        must.append(dma("sa"[k % 2], T.osc[4 * k:4 * k + 4, :], st[32 * k:32 * k + 4, :], tq, ""))
+    must.append(dma("s", T.y[:, H:C], T.yb[:], "yb", ""))
+    add("g", None, "", "", also=must)
+    emit(g, T, ops)

@@ -4,14 +4,18 @@ Op, Fn = AluOpType, ActivationFunctionType
 C, R = 384, 3
 H = C // 2
 PARTNER = [1, 2, 1]
-UP = 2.0 ** 20
-NIL = 2.0 ** -100
-NA = {1: 576, 2: 512, 3: 512, 4: 464, 5: 464, 6: 464, 8: 496}
+LO = 2.0 ** -59
+EPS = 1 + 2.0 ** -15
+NA = {3: 500, 4: 464, 5: 464, 6: 464, 7: 464}
+ND = {1: (C + H, C), 2: (C, C)}
 EMPTY, HOLD = 512, 4096.0
 SLOTS = 2 * C + 2
 DUMP = 2 * C + 8
 WIN = DUMP + 128 * 24 + 2 * C
-F32, BF, U16, I32, Q, U8 = "float32", "bfloat16", "uint16", "int32", "float8_e4m3fn_x4", "uint8"
+F32, BF, F16, U16, I32, Q, U8 = "float32", "bfloat16", "float16", "uint16", "int32", "float8_e4m3fn_x4", "uint8"
+TAIL = ("zg20v zg10v zg30a zg31v zg00a zq0v pw310p zg11a zg01v pw100p zg21a zq1v ev310a pw200p ev100v pw300p ev300a "
+        "ev200v pw201p pd311p ev210v ev211v ev201v ev110v pw311p pw000p ev010v ev000v pw101p pw001p ev101v pd301p "
+        "ev111v ev311a pw301p ev001v ev011v tg21a tg11v tg00v tg01v tg20a ev301a tg10a tg30a tg31a tq0v tq1v").split()
 
 
 def sb(n, d):
@@ -21,20 +25,22 @@ def sb(n, d):
 SCRATCH = {
     "xt": sb(4 * C, BF), "tt": sb(4 * C, BF), "zt": sb(4 * C, BF), "ut": sb(512, BF), "vt": sb(512, BF),
     "qu": sb(128, Q), "su": sb(128, U8), "qp": sb(256, Q), "sp": sb(256, U8), "qv": sb(128, Q), "sv": sb(128, U8),
-    "qw": sb(512, Q), "sw": sb(512, U8), "qz": sb(C, Q), "sz": sb(C, U8), "qe": sb(1024, Q), "se": sb(1024, U8),
+    "qw": sb(512, Q), "sw": sb(512, U8), "qz": sb(C, Q), "sz": sb(C, U8), "qe": sb(640, Q), "se": sb(640, U8),
     "ep": sb(516, BF), "en": sb(516, BF),
     "ip": sb(1, I32), "ip2": sb(1, I32), "iu": sb(16, I32), "ou": sb(16, U16), "i49": sb(49, F32),
-    "col": sb(32, F32), "lo2": sb(2, BF), "oh": sb(16, F32), "tri": sb(16, F32), "c64": sb(17, F32), "c2": sb(17, F32),
-    "g12": sb(17, F32), "g2": sb(17, F32), "tmp": sb(32, F32), "t1": sb(18, F32), "t2": sb(18, F32), "wm": sb(18, F32),
-    "ctab": sb(48, F32), "wn": sb(48, F32), "off": sb(2, U16), "gat": sb(32, F32), "gat2": sb(32, F32),
-    "xx": sb(2 * C, F32), "yy": sb(2 * C, F32), "rr": sb(2 * C, F32), "nz": sb(C, F32), "ab": sb(C, F32),
-    "sg": sb(C, F32), "mm": sb(C, F32), "rg": sb(C, F32), "junk": sb(2 * C, BF), "fl": sb(304, BF), "sc": sb(152, BF),
+    "col": sb(40, F32), "lo": sb(2, BF), "oh": sb(16, F32), "tri": sb(16, F32), "c4": sb(33, F32),
+    "g16": sb(33, F32), "tmp": sb(32, F32), "t1a": sb(34, F32), "t1b": sb(34, F32), "c8": sb(34, F32),
+    "u0": sb(34, F32), "t2": sb(34, F32), "wm": sb(34, F32), "wu": sb(34, F32),
+    "ctab": sb(40, F32), "wn": sb(40, F32), "off": sb(2, U16), "ofd": sb(2, U16), "gat": sb(32, F32), "gat2": sb(32, F32),
+    "xx": sb(2 * C, F32), "yy": sb(2 * C, F32), "rr": sb(2 * C, F32), "nz": sb(C, F32), "ab": sb(C, F32), "ck": sb(H, BF),
+    "sg": sb(C, F32), "mm": sb(C, F32), "rg": sb(C, F32), "junk": sb(2 * C, BF), "junk2": sb(2 * C, BF),
+    "fla": sb(C, BF), "flb": sb(C, BF), "sca": sb(H, F16), "scb": sb(H, F16),
     "bd": sb(24, F32), "sd": sb(24, F32), "rd": sb(48, F32), "xd": sb(48, F32), "yd": sb(48, F32), "ye": sb(24, F32),
     "ae": sb(100, F32), "keep": sb(100, F32), "pp": sb(100, F32), "o2": sb(2, U16), "tab": sb(3 * 784, BF),
     "w1": sb(24, F32), "w2": sb(24, F32), "za": sb(24, F32), "h0": sb(96, F32), "h1": sb(96, F32), "hs": sb(96, F32),
     "osl": sb(24, U16), "val": sb(C, BF), "win": sb(WIN, BF), "i16": sb(400, BF), "dk": sb(800, BF),
-    "sk": sb(SLOTS, "float16"), "mk": sb(24, F32), "ok": sb(24, U16),
-    "dd": sb(4 * C, BF), "ff": sb(8 * C, BF), "i768": sb(2 * C, F32), "kr": sb(C, F32), "mr": sb(C, F32),
+    "sk": sb(SLOTS, F16), "mk": sb(24, F32), "ok": sb(24, U16),
+    "dd": sb(4 * C, BF), "dn": sb(3 * C, BF), "ff": sb(8 * C, BF), "i768": sb(2 * C, F32), "kr": sb(C, F32),
     "ya": sb(H, F32), "yb": sb(H, F32),
 }
 for _t in range(R + 1):
@@ -48,7 +54,7 @@ for _t in range(R):
 for _b in range(8):
     SCRATCH["ps%d" % _b] = ("psum", [128, 512], F32)
 
-POOL = {"v": 36, "a": 36, "p": 20, "g": 20, "d": 24}
+POOL = {"v": 40, "a": 34, "p": 22, "g": 20, "d": 22}
 SEMAPHORES = ["%s%d" % (k, i) for k in POOL for i in range(POOL[k])]
 SEMAPHORES += ["%s%d" % (k, t) for k in ("aq", "al", "sq", "sl") for t in range(R)]
 
@@ -162,6 +168,11 @@ def rank_program(g, core, T, topo):
     def acopy(out, in_, r, w):
         return add("a", lambda e: e.activation(out, in_, Fn.Copy), r, w)
 
+    def times(q, out, in_, c, r, w):
+        if q == "v":
+            return ts(out, in_, c, Op.mult, r, w)
+        return act(out, in_, Fn.Copy, r, w, scale=c)
+
     def iota(out, pat, base, cm, w, small=True):
         if small:
             return add("g", lambda e: e.iota(out, pat, base, cm, allow_small_or_imprecise_dtypes=True), "", w)
@@ -183,7 +194,7 @@ def rank_program(g, core, T, topo):
     def arrival(src, name, writes, w):
         must.append(add("x", None, "", w, sem=(name, len(topo.engines(src, core)) * writes)))
 
-    names = ["pm", "pm1", "pw", "f", "ipw", "rc", "f2", "th1", "th2", "th3", "th7", "thy", "ts", "nacc", "beta", "gam"]
+    names = ("pm pma pmb phi q4 q128 c1 low inv kap cf a32 th1a th1b th2a th2b u u2 th6 ts na nb beta gam f base").split()
     col = {n: T.col[:, i:i + 1] for i, n in enumerate(names)}
     u8 = dt.uint8
 
@@ -199,44 +210,59 @@ def rank_program(g, core, T, topo):
     iota(T.i49[:], [[1, 49]], 0, 0, "i49")
     fill(T.ep[:], 64.0, "ep")
     fill(T.en[:], -64.0, "en")
-    fill(T.c64[:], 64.0, "c64")
-    fill(T.c2[:], 2.0, "c2")
+    fill(T.c4[:], 4.0, "c4")
     for n in ("ep", "en"):
         if n == "en":
             iota(T.i16[:], [[0, 25], [1, 16]], 0, 0, "i16")
         add("g", lambda e, n=n: e.affine_select(T[n][:], T[n][:], [[1, 516]], Op.is_equal, 0.0, -3, -4), n, n)
     ts(T.ip2[:], T.ip[:], 15, Op.bitwise_and, "ip", "ip2")
     cp(T.ou[:], T.iu[:], "iu", "ou")
-    scan(T.g12[:], T.c64[:], T.c64[:], NIL / 4096.0, Op.mult, Op.mult, "c64", "g12")
+    scan(T.g16[:], T.c4[:], T.c4[:], LO / 16, Op.mult, Op.mult, "c4", "g16")
     cp(col["pm"], T.ip2[:], "ip2", "pm")
-    scan(T.g2[:], T.c2[:], T.c2[:], 1.0, Op.mult, Op.max, "c2", "g2")
+    joint("eighths")
+    fill(T.u0[:], 0.0, "u0")
+    for k in range(4):
+        fill(T.c8[:, 1 + 8 * k:9 + 8 * k], 2.0 ** k / 8, "c8%d" % k)
+    for n in ("t1a", "t1b", "wm"):
+        fill(T[n][:, 0:1], 0.0, n + "0")
+    joint(None)
     ts(T.oh[:], T.i49[:, 0:16], col["pm"], Op.is_equal, "i49 pm", "oh")
     ts(T.tri[:], T.i49[:, 0:16], col["pm"], Op.is_lt, "i49 pm", "tri")
-    ts(T.off[:, 1:2], col["pm"], 2.0, Op.add, "pm", "off1", 4.0, Op.min)
-    tt(T.tmp[:, 0:16], T.g12[:, 1:17], T.oh[:], Op.mult, "g12 oh", "tmpa")
-    tt(T.tmp[:, 16:32], T.g2[:, 0:16], T.oh[:], Op.mult, "g2 oh", "tmpb")
-    act(col["pm1"], col["pm"], Fn.Identity, "pm", "pm1", bias=1.0)
-    act(col["f"], col["pm"], Fn.Identity, "pm", "f", bias=17.0 / 16, scale=1.0 / 16)
-    act(col["f2"], col["pm"], Fn.Identity, "pm", "f2", bias=17.0 / 32, scale=1.0 / 32)
-    red(col["th1"], T.tmp[:, 0:16], Op.add, "tmpa", "th1")
-    red(col["pw"], T.tmp[:, 16:32], Op.add, "tmpb", "pw")
-    add("v", lambda e: e.reciprocal(T.col[:, 4:6], T.col[:, 2:4]), "pw f", "ipw rc")
-    ts(T.t1[:, 1:17], T.g12[:, 1:17], col["pw"], Op.mult, "g12 pw", "t1")
-    act(T.t1[:, 0:1], col["pm"], Fn.Identity, "pm", "t1a", scale=0.0)
-    act(T.t1[:, 17:18], col["pw"], Fn.Identity, "pw", "t1b", scale=NIL / 16)
-    act(T.t2[:, 0:1], col["pm"], Fn.Identity, "pm", "t2a", scale=0.0)
-    act(T.t2[:, 17:18], col["f"], Fn.Identity, "f", "t2b", scale=1.0 / 16)
-    ts(T.t2[:, 1:17], T.g2[:, 0:16], col["f2"], Op.mult, "g2 f2", "t2")
-    act(T.ctab[:], T.i49[:, 0:48], Fn.Identity, "i49", "ctab0", scale=0.0)
-    steps = [2.0 ** -4, 2.0 ** -8, 2.0 ** -12, 2.0 ** -16, 2.0 ** -20, 2.0 ** -23]
-    cells = [(8 * k + 1, 0.0, steps[k]) for k in range(6)]
-    cells += [(8 * k + 3, steps[k + 1] - steps[k], steps[k + 1] - steps[k]) for k in range(4)]
-    cells += [(2, 1.0 / 16, 17.0 / 16), (35, steps[5] - steps[4], steps[5] / 2 - steps[4]), (45, steps[5], steps[5] / 2)]
+    ts(T.tmp[:, 16:17], col["pm"], -1.0, Op.mult, "pm", "tmpb", 4.0, Op.add)
+    ts(T.u0[:, 8:33:8], T.c8[:, 8:33:8], 8.0, Op.mult, "u0 c80 c81 c82 c83", "u8")
+    fill(T.u0[:, 33:34], 1.0 / 32, "u0")
+    tt(T.tmp[:, 0:16], T.g16[:, 1:17], T.oh[:], Op.mult, "g16 oh", "tmpa")
+    ts(T.off[:, 1:2], T.tmp[:, 16:17], 2.0, Op.max, "tmpb", "off1")
+    joint("cols")
+    for n, a, b in (("pma", 1.0, 1.0), ("pmb", 1.0, 17.0), ("q4", 0.25, 0.25), ("q128", 1.0 / 128, 1.0 / 128),
+                    ("c1", 0.125, 1.125), ("low", LO * EPS / 4, LO * EPS / 4), ("cf", -LO / 4096, LO * 127 / 4096),
+                    ("a32", 1.0 / 4096, 129.0 / 4096)):
+        act(col[n], col["pm"], Fn.Identity, "pm", n, bias=b, scale=a)
+    joint(None)
+    red(col["th1a"], T.tmp[:, 0:16], Op.add, "tmpa", "th1a")
+    tt(col["phi"], col["c1"], col["q4"], Op.max, "c1 q4", "phi")
+    ts(T.t2[:, 1:33], T.u0[:, 1:33], col["q128"], Op.mult, "u0 u8 q128", "t2")
+    ts(col["th1b"], col["th1a"], 2.0 ** 64, Op.mult, "th1a", "th1b")
+    ts(T.t1a[:, 2:33], T.g16[:, 2:33], col["phi"], Op.mult, "g16 phi", "t1a2", EPS * 15 / 16, Op.mult)
+    ts(T.t1b[:, 1:33], T.g16[:, 1:33], col["phi"], Op.mult, "g16 phi", "t1b1", EPS * 15 / 4, Op.mult)
+    ts(T.t1a[:, 1:2], col["phi"], 16 * LO * EPS, Op.mult, "phi low", "t1a1", col["low"], Op.subtract)
+    tt(T.t2[:, 1:33], T.t2[:, 1:33], T.c8[:, 1:33], Op.add, "t2 c80 c81 c82 c83", "t2")
+    add("v", lambda e: e.reciprocal(col["inv"], col["phi"]), "phi", "inv")
+    act(T.t1a[:, 33:34], col["low"], Fn.Identity, "low", "t1a3", scale=1.0 / 32)
+    act(T.t1b[:, 33:34], col["phi"], Fn.Identity, "phi", "t1b3", scale=LO * EPS / 8)
+    act(col["kap"], col["phi"], Fn.Identity, "phi", "kap", scale=16 * LO)
+    act(T.ctab[:], T.i49[:, 0:40], Fn.Identity, "i49", "ctab0", scale=0.0)
+    steps = {3: 2.0 ** -7, 4: 2.0 ** -11, 5: 2.0 ** -15, 6: 2.0 ** -19, 7: 2.0 ** -23}
+    at = {k: 8 * ((k + 1) % 5) for k in steps}
+    cells = [(at[k] + 1, 0.0, steps[k]) for k in steps]
+    cells += [(at[k] + 3, steps[k + 1] - steps[k], steps[k + 1] - steps[k]) for k in (3, 4, 5)]
+    cells += [(at[6] + 3, steps[7] - steps[6], steps[7] / 2 - steps[6]), (at[7] + 3, -steps[7], -steps[7] / 2)]
     joint("cells")
     for c, a, b in cells:
         act(T.ctab[:, c:c + 1], col["pm"], Fn.Identity, "pm ctab0", "ctab%d" % (c + 1), bias=b, scale=a)
     joint(None)
     ctab = " ".join("ctab%d" % (c + 1) for c, a, b in cells)
+    th = {k: T.wn[:, at[k] + 4:at[k] + 5] for k in steps}
 
     def late_g():
         iota(T.ae[:], [[0, 100]], 0, 0, "ae0")
@@ -257,124 +283,169 @@ def rank_program(g, core, T, topo):
     tab1 = " ".join("tab1_%d" % i for i in range(16))
 
     def qe(k):
-        src, b = ("ep", "en")[k // 4], k % 4
+        src, b = ("ep", "en")[k // 4], min(k, 3)
         quant(T.qe[:, 128 * k:128 * k + 128], T.se[:, 128 * k:128 * k + 128], T[src][:, 3 - b:515 - b], src, "qe%d" % k)
+
+    def unpack(bank, k, qt, st, r, stop=True):
+        mx(bank, qt[1] - qt[0], T.qe[:, 128 * k:128 * k + 128], T.se[:, 128 * k:128 * k + 128],
+           T["%s" % st[0]][:, qt[0]:qt[1]], T["%s" % st[1]][:, qt[0]:qt[1]], True, stop, "qe%d %s" % (k, r))
 
     def hold(out, c, w):
         ts(out, T.i16[:], col["pm"], Op.is_equal, "i16 pm", w, c, Op.mult)
 
-    def halves(k, tile, ra, rb):
-        quant(T["qt%d" % k][:, 0:H], T["st%d" % k][:, 0:H], tile[:, 0:4 * H], ra, "qt%da" % k)
-        quant(T["qt%d" % k][:, H:C], T["st%d" % k][:, H:C], tile[:, 4 * H:4 * C], rb, "qt%db" % k)
+    def half(k, tile, h, r):
+        a = H * h
+        quant(T["qt%d" % k][:, a:a + H], T["st%d" % k][:, a:a + H], tile[:, 4 * a:4 * a + 4 * H], r, "qt%d%d" % (k, h))
 
     qe(0)
     qe(1)
     quant(T.qu[:], T.su[:], T.ut[:], "ut", "qu")
     acopy(T.sp[:], T.su[:].indirect(T.ou[:]), "qu ou", "sp")
     cp(T.qp[:].bitcast(dt.uint32), T.qu[:].bitcast(dt.uint32).indirect(T.ou[:]), "qu ou", "qp")
-    tri_a(0, 14)
-    halves(0, T.xt, "xta", "xtb")
+    tri_a(0, 12)
+    half(0, T.xt, 0, "xta")
+    half(0, T.xt, 1, "xtb")
 
     def rest_a():
-        tri_a(14, 16)
+        tri_a(12, 16)
         dma("s", T.tab[:, 1568:2352], T.tab[:, 784:1568], tab1, "tab2")
 
     def ends_a():
         act(T.ae[:, 49:50], col["pm"], Fn.Identity, "pm ae0", "ae49", scale=49.0)
         act(T.ae[:, 99:100], col["pm"], Fn.Identity, "pm ae0", "ae99", scale=49.0, bias=784.0)
 
-    idle_v = {(0, 1): lambda: hold(T.dk[:, 0:800:2], HOLD, "dk0"), (0, 2): lambda: hold(T.dk[:, 1:800:2], 0.5, "dk1"),
-              (0, 3): lambda: qe(2), (0, 4): lambda: qe(3), (0, 5): lambda: qe(4),
+    idle_v = {(0, 2): lambda: (hold(T.dk[:, 0:800:2], HOLD, "dk0"), hold(T.dk[:, 1:800:2], 0.5, "dk1")),
+              (0, 3): lambda: (qe(2), qe(3), qe(4)),
               (1, 3): lambda: quant(T.qv[:], T.sv[:], T.vt[:], "vt", "qv")}
-    idle_a = {(0, 1): rest_a, (0, 3): ends_a}
+    idle_a = {(0, 2): rest_a, (0, 3): ends_a}
 
     for t in range(R):
         mate = T.cores[rank ^ PARTNER[t]]
         qt, st, lq, ls, oa, la = (T["%s%d" % (n, t)] for n in ("qt", "st", "lq", "ls", "oa", "la"))
-        tq = "qt%da qt%db" % (t, t)
-        mx(0, H, T.qp[:, 128:256], T.sp[:, 128:256], qt[:, 0:H], st[:, 0:H], True, True, "qp sp qt%da" % t)
-        mx(2, H, T.qp[:, 128:256], T.sp[:, 128:256], qt[:, H:C], st[:, H:C], True, True, "qp sp qt%db" % t)
-        mx(1, C, T.qp[:, 0:128], T.sp[:, 0:128], qt[:], st[:], True, True, "qp sp " + tq)
+        tq = "qt%d0 qt%d1" % (t, t)
+        own, far = ("qt%d" % t, "st%d" % t), ("lq%d" % t, "ls%d" % t)
+        mx(0, H, T.qp[:, 128:256], T.sp[:, 128:256], qt[:, 0:H], st[:, 0:H], True, True, "qp sp qt%d0" % t)
+        mx(1, H, T.qp[:, 128:256], T.sp[:, 128:256], qt[:, H:C], st[:, H:C], True, True, "qp sp qt%d1" % t)
+        mx(2, C, T.qp[:, 0:128], T.sp[:, 0:128], qt[:], st[:], True, True, "qp sp " + tq)
         send([(lq[:].bitcast(u8), qt[:].bitcast(u8)), (ls[:], st[:])], mate, "aq%d" % t, "sq%d" % t, tq)
         arrival(mate, "aq%d" % t, 2, "lq%d" % t)
         if t == 0:
             late_g()
         if t == 1:
             iota(T.i768[:], [[1, 2 * C]], 0, 0, "i768")
-        for a, bank, n in ((0, 0, "a"), (H, 2, "b")):
-            z = T["ps%d" % bank][:, 0:H]
-            if t == 0:
-                ts(T.xx[:, a:a + H], z, -UP, Op.mult, "ps%d" % bank, "xb" + n, NIL, Op.max)
-            else:
-                act(T.nz[:, a:a + H], z, Fn.Relu, "ps%d" % bank, "nz" + n, scale=-UP)
-                tt(T.xx[:, a:a + H], T.mm[:, a:a + H], T.nz[:, a:a + H], Op.add, "mm nz" + n, "xb" + n)
-        act(T.ab[:], T.ps1[:, 0:C], Fn.Abs, "ps1", "ab", scale=UP)
-        tt(T.xx[:, C:C + H], T.xx[:, 0:H], T.ab[:, 0:H], Op.add, "xba ab", "xc")
-        tt(T.xx[:, C + H:2 * C], T.xx[:, H:C], T.ab[:, H:C], Op.add, "xbb ab", "xe")
-        act(T.sg[:], T.ps1[:, 0:C], Fn.Copy, "ps1", "sg", scale=UP)
-        dma("s", T.bd[:], T.xx[0:128:16, 0:C], "xba xbb", "bd")
-        dma("s", T.sd[:], T.sg[0:128:16, :], "sg", "sd")
+        if t == 0:
+            for h in range(2):
+                ts(T.xx[:, H * h:H * h + H], T["ps%d" % h][:, 0:H], -1.0, Op.mult, "ps%d" % h, "x%d" % h, 0.0, Op.max)
+        else:
+            ts(T.nz[:, 0:H], T.ps0[:, 0:H], -1.0, Op.mult, "ps0", "nz0", 0.0, Op.max)
+            act(T.nz[:, H:C], T.ps1[:, 0:H], Fn.Relu, "ps1", "nz1", scale=-1.0)
+            for h in range(2):
+                a = H * h
+                tt(T.xx[:, a:a + H], T.mm[:, a:a + H], T.nz[:, a:a + H], Op.add, "mm nz%d" % h, "x%d" % h)
+        act(T.ab[:], T.ps2[:, 0:C], Fn.Abs, "ps2", "ab")
+        tt(T.xx[:, C:C + H], T.xx[:, 0:H], T.ab[:, 0:H], Op.add, "x0 ab", "x2")
+        tt(T.ck[:], T.xx[:, H:C], T.ab[:, H:C], Op.add, "x1 ab", "ck")
+        dma("s", T.bd[:], T.xx[0:128:16, 0:C], "x0 x1", "bd")
+
+        def signs():
+            act(T.sg[:], T.ps2[:, 0:C], Fn.Copy, "ps2", "sg")
+            dma("s", T.sd[:], T.sg[0:128:16, :], "sg", "sd")
+
+        def less(h):
+            a = C * h
+            ts(T.yy[:, a:a + C], T.xx[:, a:a + C], th[4], Op.subtract, "x%d x%d th4" % (2 * h, 2 * h + 1), "y%d" % h)
+
+        def spread():
+            tt(T.xd[:, 0:48:2], T.bd[:], T.rd[:, 0:48:2], Op.add, "bd rd0", "xd0")
+            tt(T.xd[:, 1:48:2], T.bd[:], T.rd[:, 1:48:2], Op.add, "bd rd1", "xd1")
+            ts(T.ye[:], T.bd[:], th[4], Op.subtract, "bd th4", "ye")
+            ts(T.yd[:], T.xd[:], th[4], Op.subtract, "xd0 xd1 th4", "yd")
+
+        idle_a[t, 1] = signs
         idle_a[t, 5] = lambda: (act(T.rd[:, 0:48:2], T.sd[:], Fn.Relu, "sd", "rd0", scale=-1.0),
                                 act(T.rd[:, 1:48:2], T.sd[:], Fn.Relu, "sd", "rd1"))
+        idle_v[t, 1] = lambda: tt(T.xx[:, C + H:2 * C], T.xx[:, H:C], T.ab[:, H:C], Op.add, "x1 ab", "x3")
+        idle_v[t, 4] = lambda: less(0)
+        idle_v[t, 5] = lambda: less(1)
+        idle_v[t, 6] = spread
 
-        def count(k, data, tok_a, tok_v, th, tth, between=None, behind=None):
+        def quarters(name, lo, hi):
+            return " ".join("%s%d" % (name, i) for i in range(lo // H, (hi - 1) // H + 1))
+
+        def double(k, between, behind):
+            both = list(zip("ba", ND[k][::-1], (T.junk2, T.junk), (T.flb, T.fla), (T.scb, T.sca)))
+            for n, na, junk, fl, sc in both:
+                act(junk[:, 0:na], T.xx[:, 0:na], Fn.Sign, quarters("x", 0, na) + " th%d%s" % (k, n), "n%s junk%s" % (n, n),
+                    bias=col["th%d%s" % (k, n)], scale=-1.0, acc=col["n" + n])
+            idle_a.get((t, k), lambda: 0)()
+            for n, na, junk, fl, sc in both:
+                m, c = C + H - na, col["th%d%s" % (k, n)]
+                if m:
+                    ts(fl[:, 0:m], T.xx[:, na:C + H], c, Op.is_gt, quarters("x", na, C + H) + " th%d%s" % (k, n), "fl0" + n,
+                       2.0, Op.mult)
+                ts(fl[:, m:m + H], T.ck[:], c, Op.is_gt, "ck th%d%s" % (k, n), "fl1" + n, 2.0, Op.mult)
+            between()
+            for n, na, junk, fl, sc in both:
+                nv = 2 * C - na
+                scan(sc[:, 0:nv // 2], fl[:, 0:nv // 2], fl[:, nv // 2:nv], -float(nv), Op.add, Op.add,
+                     "fl0%s fl1%s" % (n, n), "sc" + n)
+            behind()
+            for n, na, junk, fl, sc in both:
+                nv, i = 2 * C - na, "ab".index(n)
+                ts(T.ofd[:, i:i + 1], sc[:, nv // 2 - 1:nv // 2], col["n" + n], Op.is_gt, "sc%s n%s pm%s" % (n, n, n),
+                   "ofd" + n, col["pm" + n], Op.mult)
+
+        def climb(out, table, bias, acc, r, w):
+            act(T[out][:], table[:, 0:33].indirect(T.ofd[:]), Fn.Identity, "ofda ofdb " + r, out + " " + w, bias=bias, acc=acc)
+
+        def count(k, data, name, c, tc, between=None, behind=None):
             na = NA[k]
-            act(T.junk[:, 0:na], data[:, 0:na], Fn.Sign, tok_a + " " + tth, "nacc junk", bias=th, scale=-1.0, acc=col["nacc"])
+            n = H if name == "x" else C
+            toks = [" ".join("%s%d" % (name, i) for i in range(lo // n, (hi - 1) // n + 1)) for lo, hi in ((0, na), (na, 2 * C))]
+            act(T.junk[:, 0:na], data[:, 0:na], Fn.Sign, toks[0] + " " + tc, "na junka", bias=c, scale=-1.0, acc=col["na"])
             idle_a.get((t, k), lambda: 0)()
             nv = 2 * C - na
-            ts(T.fl[:, 0:nv], data[:, na:2 * C], th, Op.is_gt, tok_v + " " + tth, "fl", 2.0, Op.mult)
+            ts(T.fla[:, 0:nv], data[:, na:2 * C], c, Op.is_gt, toks[1] + " " + tc, "fl0a fl1a", 2.0, Op.mult)
             if between:
                 between()
-            scan(T.sc[:, 0:nv // 2], T.fl[:, 0:nv // 2], T.fl[:, nv // 2:nv], -float(nv), Op.add, Op.add, "fl", "sc")
+            scan(T.sca[:, 0:nv // 2], T.fla[:, 0:nv // 2], T.fla[:, nv // 2:nv], -float(nv), Op.add, Op.add, "fl0a fl1a", "sca")
             if behind:
                 behind()
-            last = T.sc[:, nv // 2 - 1:nv // 2]
-            if k <= 2:
-                ts(T.off[:, 0:1], last, col["nacc"], Op.is_gt, "sc nacc pm1", "off0", col["pm1"], Op.mult)
-            else:
-                ts(T.off[:, 0:1], last, col["nacc"], Op.is_gt, "sc nacc", "off0")
+            ts(T.off[:, 0:1], T.sca[:, nv // 2 - 1:nv // 2], col["na"], Op.is_gt, "sca na", "off0")
 
-        def climb(k, table, r, w):
-            act(T.gat2[:, 0:16], table[:, 0:17].indirect(T.off[:, 0:1]), Fn.Identity, "off0 " + r, "gat2 " + w,
-                bias=table[:, 17:18], acc=col[w])
+        def step(k, out, r, w):
+            act(T.gat2[:], T.wn[:, at[k]:at[k] + 5].indirect(T.off[:]), Fn.Identity, "off0 off1 wn " + r, "gat2 " + w, acc=out)
             idle_v.get((t, k), lambda: 0)()
 
-        def step(k, out, w):
-            a = 8 * (k - 3)
-            act(T.gat2[:], T.wn[:, a:a + 5].indirect(T.off[:]), Fn.Identity, "off0 off1 wn wn%d" % k, "gat2 " + w, acc=out)
-            idle_v.get((t, k), lambda: 0)()
-
-        count(1, T.xx, "xba xbb xc", "xe", col["th1"], "th1")
-        climb(1, T.t1, "t1 t1a t1b", "th2")
-        count(2, T.xx, "xba xbb xc", "xc xe", col["th2"], "th2",
-              lambda: ts(T.lo2[:, 1:2], col["th2"], col["ipw"], Op.mult, "th2 ipw", "lo1"),
-              lambda: ts(T.wm[:], T.t2[:], T.lo2[:, 1:2], Op.mult, "lo1 t2 t2a t2b", "wm"))
-        climb(2, T.wm, "wm", "th3")
-        count(3, T.xx, "xba xbb xc", "xc xe", col["th3"], "th3",
-              lambda: ts(T.lo2[:, 0:1], col["th3"], col["rc"], Op.mult, "th3 rc", "lo2"),
-              lambda: ts(T.wn[:], T.ctab[:], T.lo2[:, 0:1], Op.mult, "lo2 ctab0 " + ctab, "wn wn3 wn4 wn5 wn6 wn7 wn8"))
-        step(3, T.wn[:, 10:11], "wn4")
-        count(4, T.xx, "xba xbb xc", "xc xe", T.wn[:, 10:11], "wn4")
-        step(4, T.wn[:, 18:19], "wn5")
-        count(5, T.xx, "xba xbb xc", "xc xe", T.wn[:, 18:19], "wn5")
-        step(5, T.wn[:, 26:27], "wn6")
-        count(6, T.xx, "xba xbb xc", "xc xe", T.wn[:, 26:27], "wn6")
-        step(6, col["th7"], "th7")
-        tt(T.xd[:, 0:48:2], T.bd[:], T.rd[:, 0:48:2], Op.add, "bd rd0", "xd0")
-        tt(T.xd[:, 1:48:2], T.bd[:], T.rd[:, 1:48:2], Op.add, "bd rd1", "xd1")
-        act(T.junk[:], T.xx[:], Fn.Sign, "xba xbb xc xe th7", "nacc junk", bias=col["th7"], scale=-1.0, acc=col["nacc"])
-        ts(T.yy[:], T.xx[:], col["th7"], Op.subtract, "xba xbb xc xe th7", "yy")
-        ts(T.off[:, 0:1], col["nacc"], 0.0, Op.is_lt, "nacc", "off0")
-        step(7, col["thy"], "thy")
-        ts(T.yd[:], T.xd[:], col["th7"], Op.subtract, "xd0 xd1 th7", "yd")
-        ts(T.ye[:], T.bd[:], col["th7"], Op.subtract, "bd th7", "ye")
-        count(8, T.yy, "yy", "yy", col["thy"], "thy",
-              lambda: ts(T.wn[:, 42:43], col["thy"], T.wn[:, 45:46], Op.subtract, "thy wn", "wn8"))
-        step(8, col["ts"], "ts")
+        double(1, lambda: 0, lambda: 0)
+        climb("gat", T.t1b, T.t1b[:, 33:34], col["th2b"], "t1b0 t1b1 t1b3", "th2b")
+        climb("gat2", T.t1a, T.t1a[:, 33:34], col["th2a"], "t1a0 t1a1 t1a2 t1a3", "th2a")
+        idle_v[t, 1]()
+        double(2, lambda: (ts(T.lo[:, 0:1], col["th2b"], col["inv"], Op.mult, "th2b inv", "lo", 0.25, Op.mult),
+                           ts(col["f"], col["th2b"], col["kap"], Op.is_lt, "th2b kap cf", "f", col["cf"], Op.mult)),
+               lambda: (ts(T.wm[:, 1:33], T.t2[:, 1:33], T.lo[:, 0:1], Op.mult, "lo t2", "wm1", LO / 4, Op.max),
+                        ts(col["base"], T.lo[:, 0:1], col["a32"], Op.mult, "lo a32 f", "base", col["f"], Op.subtract),
+                        ts(T.wu[:], T.u0[:], T.lo[:, 0:1], Op.mult, "lo u0 u8", "wu")))
+        climb("gat", T.wm, col["base"], th[3], "wm0 wm1 base", "th3")
+        climb("gat2", T.wu, T.wu[:, 33:34], col["u"], "wu", "u")
+        idle_v.get((t, 2), lambda: 0)()
+        count(3, T.xx, "x", th[3], "th3",
+              lambda: ts(col["u2"], col["u"], 2 * LO, Op.max, "u", "u2"),
+              lambda: ts(T.wn[:, 0:36], T.ctab[:, 0:36], col["u2"], Op.mult, "u2 ctab0 " + ctab, "wn th4 th5 w6 th7"))
+        step(3, th[4], "th3", "th4")
+        count(4, T.xx, "x", th[4], "th4")
+        step(4, th[5], "th4", "th5")
+        count(5, T.xx, "x", th[5], "th5")
+        step(5, col["th6"], "th5", "th6")
+        count(6, T.xx, "x", col["th6"], "th6", lambda: ts(th[6], col["th6"], th[4], Op.subtract, "th6 th4", "w6"))
+        step(6, th[7], "w6", "th7")
+        count(7, T.yy, "y", th[7], "th7")
+        step(7, col["ts"], "th7", "ts")
 
         for b in range(4):
-            mx(2 + b, C, T.qe[:, 128 * b:128 * b + 128], T.se[:, 128 * b:128 * b + 128], lq[:], ls[:], True, True,
-               "qe%d lq%d" % (b, t))
+            unpack(4 + b, b, (0, C), far, "lq%d" % t)
+        for b in range(3):
+            unpack(b + b // 2, b, (0, C), own, tq)
 
         ts(T.ae[:, 1:49], T.yd[:], col["ts"], Op.is_lt, "yd ts ae0", "aea")
         ts(T.ae[:, 51:99], T.yd[:], col["ts"], Op.is_equal, "yd ts ae0", "aee")
@@ -391,7 +462,7 @@ def rank_program(g, core, T, topo):
         ts(T.h1[:, 1:96:2], T.pp[:, 51:99], col["beta"], Op.min, "pp beta", "h1b")
         ts(T.h1[:, 0:96:4], T.za[:], col["beta"], Op.is_ge, "za beta", "h1a")
         for b in range(4):
-            act(T.dd[:, C * b:C * b + C], T["ps%d" % (2 + b)][:, 0:C], Fn.Copy, "ps%d" % (2 + b), "dd%d" % b, scale=1.0 / 64)
+            act(T.dd[:, C * b:C * b + C], T["ps%d" % (4 + b)][:, 0:C], Fn.Copy, "ps%d" % (4 + b), "dd%d" % b, scale=1.0 / 64)
         act(T.rr[:, 0:2 * C:2], T.sg[:], Fn.Relu, "sg", "r0", scale=-1.0)
         act(T.rr[:, 1:2 * C:2], T.sg[:], Fn.Relu, "sg", "r1")
         scan(T.hs[:], T.h0[:], T.h1[:], 0.0, Op.mult, Op.add, "h0 h1a h1b h1c", "hs")
@@ -405,45 +476,51 @@ def rank_program(g, core, T, topo):
 
         ts(T.ok[:], T.mk[:], 2.0, Op.mult, "mk", "ok", float(C), Op.add)
         acopy(T.rg[:], T.rr[:].indirect(T.ok[:]), "r0 r1 ok", "rg")
-        if t == 0:
-            qe(5)
-            qe(6)
-            qe(7)
-        tt(T.mm[:], T.xx[:, 0:C].indirect(oa[:]), T.rg[:], Op.add, "xba xbb oa%d rg" % t, "mm")
+        for b in range(3):
+            k = b + b // 2
+            acopy(T.dn[:, C * b:C * b + C], T["ps%d" % k][:, 0:C], "ps%d" % k, "dn%d" % b)
+        tt(T.mm[:], T.xx[:, 0:C].indirect(oa[:]), T.rg[:], Op.add, "x0 x1 oa%d rg" % t, "mm")
         if t < R - 1:
             iota(T.win[:, 0:SLOTS], [[0, SLOTS]], EMPTY, 0, "win")
         else:
+            must.append(dma("s", T.ml[:], T.mm[0:128:16, :], "mm", ""))
             acopy(T.kr[:], T.i768[:].indirect(T.ok[:]), "i768 ok", "kr")
             must.append(dma("s", T.kl[:], T.kr[0:128:16, :], "kr", ""))
-        order = [(0, 0, 6), (2, 0, 7), (0, 1, 0), (2, 1, 1), (1, 0, 2), (3, 0, 3), (1, 1, 4), (3, 1, 5)]
-        for b, s, bank in order:
-            k = 4 * s + b
-            mx(bank, C, T.qe[:, 128 * k:128 * k + 128], T.se[:, 128 * k:128 * k + 128], qt[:], st[:], True, False,
-               "qe%d %s" % (k, tq))
+        for s in range(2):
+            unpack(6 + s, 3 + s, (0, H), own, "qt%d0" % t, False)
 
-        for b in range(4):
-            (cp, acopy)[b // 2](T.zt[:, b:4 * C:4], T.dd[:, C * b:C * b + C].indirect(la[:]), "dd%d la%d" % (b, t), "zt%d" % b)
-        quant(T.qz[:], T.sz[:], T.zt[:], "zt0 zt1 zt2 zt3", "qz")
-        for b, s, bank in order:
-            mx(bank, C, T.qw[:, 128 * b:128 * b + 128], T.sw[:, 128 * b:128 * b + 128], T.qz[:], T.sz[:], False, True, "qw sw qz")
-        for b, s, bank in order:
-            out, src, c = T.ff[:, 2 * C * b + s:2 * C * (b + 1):2], T["ps%d" % bank][:, 0:C], (1 - 2 * s) / 64.0
-            if b < 2:
-                ts(out, src, c, Op.mult, "ps%d" % bank, "ff%d%d" % (b, s))
+        for call in TAIL:
+            kind, q, h = call[:2], call[-1], int(call[-2])
+            a, b = H * h, int(call[2])
+            s = int(call[3]) if len(call) == 6 else 0
+            bank = 6 + s if b == 3 else 2 * b + h
+            if kind == "zg":
+                (cp if q == "v" else acopy)(T.zt[:, 4 * a + b:4 * (a + H):4], T.dd[:, C * b:C * b + C].indirect(la[:, 12 * h:12 * h + 12]),
+                                            "dd%d la%d" % (b, t), "zt%d%d" % (b, h))
+            elif kind == "zq":
+                quant(T.qz[:, a:a + H], T.sz[:, a:a + H], T.zt[:, 4 * a:4 * (a + H)], " ".join("zt%d%d" % (i, h) for i in range(4)), "qz%d" % h)
+            elif kind == "pd":
+                unpack(bank, 3 + s, (a, a + H), own, "qt%d%d" % (t, h), False)
+            elif kind == "pw":
+                mx(bank, H, T.qw[:, 128 * b:128 * b + 128], T.sw[:, 128 * b:128 * b + 128], T.qz[:, a:a + H], T.sz[:, a:a + H],
+                   b < 3, True, "qw sw qz%d" % h)
+            elif kind == "ev":
+                out, src = T.ff[:, 2 * C * b + 2 * a + s:2 * C * b + 2 * (a + H):2], T["ps%d" % bank][:, 0:H]
+                if b < 3:
+                    tt(out, T.dn[:, C * b + a:C * b + a + H], src, (Op.add, Op.subtract)[s], "ps%d dn%d" % (bank, b), "ff%d%d%d" % (b, s, h))
+                else:
+                    times(q, out, src, 1.0 - 2 * s, "ps%d" % bank, "ff%d%d%d" % (b, s, h))
+            elif kind == "tg":
+                times(q, T.tt[:, 4 * a + b:4 * (a + H):4], T.ff[:, 2 * C * b:2 * C * (b + 1)].indirect(T.ok[:, 12 * h:12 * h + 12]),
+                      1.0 / 64, "ff%d00 ff%d01 ff%d10 ff%d11 ok" % (b, b, b, b), "tt%d%d" % (b, h))
             else:
-                act(out, src, Fn.Copy, "ps%d" % bank, "ff%d%d" % (b, s), scale=c)
-            if b % 2:
-                b -= 1 - s
-                (cp, acopy)[b // 2](T.tt[:, b:4 * C:4], T.ff[:, 2 * C * b:2 * C * (b + 1)].indirect(T.ok[:]),
-                                    "ff%d0 ff%d1 ok" % (b, b), "tt%d" % b)
-        halves(t + 1, T.tt, "tt0 tt1 tt2 tt3", "tt0 tt1 tt2 tt3")
+                half(t + 1, T.tt, h, " ".join("tt%d%d" % (i, h) for i in range(4)))
 
-    qt, st, tq = T["qt%d" % R], T["st%d" % R], "qt%da qt%db" % (R, R)
-    act(T.mr[:], T.mm[:], Fn.Identity, "mm", "mr", bias=-NIL / UP, scale=1.0 / UP)
-    must.append(dma("a", T.ml[:], T.mr[0:128:16, :], "mr", ""))
-    for a, bank, n in ((0, 0, "a"), (H, 1, "b")):
-        mx(bank, H, T.qv[:], T.sv[:], qt[:, a:a + H], st[:, a:a + H], True, True, "qv qt%d%s" % (R, n))
-        must.append(dma("s", T.oc[:, 4 * a:4 * a + 4 * H], qt[:, a:a + H].bitcast(u8), "qt%d%s" % (R, n), ""))
+    qt, st, tq = T["qt%d" % R], T["st%d" % R], "qt%d0 qt%d1" % (R, R)
+    for h in range(2):
+        a = H * h
+        mx(h, H, T.qv[:], T.sv[:], qt[:, a:a + H], st[:, a:a + H], True, True, "qv qt%d%d" % (R, h))
+        must.append(dma("s", T.oc[:, 4 * a:4 * a + 4 * H], qt[:, a:a + H].bitcast(u8), "qt%d%d" % (R, h), ""))
     acopy(T.ya[:], T.ps0[:, 0:H], "ps0", "ya")
     must.append(dma("a", T.y[:, 0:H], T.ya[:], "ya", ""))
     cp(T.yb[:], T.ps1[:, 0:H], "ps1", "yb")

@@ -6,16 +6,19 @@ H = C // 2
 PARTNER = [1, 2, 1]
 LO = 2.0 ** -59
 EPS = 1 + 2.0 ** -15
-NA = {3: 500, 4: 464, 5: 464, 6: 464, 7: 464}
-ND = {1: (C + H, C), 2: (C, C)}
+NA = {3: 510, 4: 490, 5: 490, 6: 490, 7: 490}
+ND = {1: (C + H, C), 2: (416, C)}
+YY = (0, 320, 640, 2 * C)
 EMPTY, HOLD = 512, 4096.0
 SLOTS = 2 * C + 2
 DUMP = 2 * C + 8
 WIN = DUMP + 128 * 24 + 2 * C
+TAB = 16 * 49
 F32, BF, F16, U16, I32, Q, U8 = "float32", "bfloat16", "float16", "uint16", "int32", "float8_e4m3fn_x4", "uint8"
-TAIL = ("zg20v zg10v zg30a zg31v zg00a zq0v pw310p zg11a zg01v pw100p zg21a zq1v ev310a pw200p ev100v pw300p ev300a "
-        "ev200v pw201p pd311p ev210v ev211v ev201v ev110v pw311p pw000p ev010v ev000v pw101p pw001p ev101v pd301p "
-        "ev111v ev311a pw301p ev001v ev011v tg21a tg11v tg00v tg01v tg20a ev301a tg10a tg30a tg31a tq0v tq1v").split()
+TAIL = ("zg30a zg10v zg20v zg00a zg11a zg31v zq0v pw100p pw210p zg01v zg21a zq1v pw000p ev100v ev110v pw310p pw300p "
+        "ev210a pw001p ev010v pw200p ev000v ev310a ev001v pw311p pw101p ev011v ev111v ev300a pw201p ev101v pd301p pw301p "
+        "ev200a ev211v ev311a ev201v tg01a tg00a ev301v tg11v tg10a tg30a tg20v tg21a tg31v tq0v tq1v").split()
+BANK = {"000": 0, "201": 0, "100": 1, "101": 1, "001": 2, "311": 3, "200": 4, "210": 5, "300": 6, "301": 6, "310": 7}
 
 
 def sb(n, d):
@@ -25,22 +28,22 @@ def sb(n, d):
 SCRATCH = {
     "xt": sb(4 * C, BF), "tt": sb(4 * C, BF), "zt": sb(4 * C, BF), "ut": sb(512, BF), "vt": sb(512, BF),
     "qu": sb(128, Q), "su": sb(128, U8), "qp": sb(256, Q), "sp": sb(256, U8), "qv": sb(128, Q), "sv": sb(128, U8),
-    "qw": sb(512, Q), "sw": sb(512, U8), "qz": sb(C, Q), "sz": sb(C, U8), "qe": sb(640, Q), "se": sb(640, U8),
+    "qw": sb(512, Q), "sw": sb(512, U8), "qz": sb(C, Q), "sz": sb(C, U8), "qe": sb(768, Q), "se": sb(768, U8),
     "ep": sb(516, BF), "en": sb(516, BF),
-    "ip": sb(1, I32), "ip2": sb(1, I32), "iu": sb(16, I32), "ou": sb(16, U16), "i49": sb(49, F32),
-    "col": sb(40, F32), "lo": sb(2, BF), "oh": sb(16, F32), "tri": sb(16, F32), "c4": sb(33, F32),
-    "g16": sb(33, F32), "tmp": sb(32, F32), "t1a": sb(34, F32), "t1b": sb(34, F32), "c8": sb(34, F32),
-    "u0": sb(34, F32), "t2": sb(34, F32), "wm": sb(34, F32), "wu": sb(34, F32),
-    "ctab": sb(40, F32), "wn": sb(40, F32), "off": sb(2, U16), "ofd": sb(2, U16), "gat": sb(32, F32), "gat2": sb(32, F32),
+    "ip": sb(1, I32), "ip2": sb(1, I32), "iu": sb(16, I32), "ou": sb(16, U16), "i16": sb(400, BF), "j16": sb(16, F32),
+    "col": sb(40, F32), "lo": sb(2, BF), "oh": sb(16, F32), "c4": sb(33, F32), "g16": sb(33, F32), "tmp": sb(16, F32),
+    "tb": sb(120, F32), "t2": sb(33, F32), "u0": sb(33, F32), "wu": sb(33, F32),
+    "ctab": sb(40, F32), "wn": sb(40, F32), "off": sb(2, U16), "ofd": sb(2, U16), "gat": sb(32, F32), "gat2": sb(48, F32),
     "xx": sb(2 * C, F32), "yy": sb(2 * C, F32), "rr": sb(2 * C, F32), "nz": sb(C, F32), "ab": sb(C, F32), "ck": sb(H, BF),
-    "sg": sb(C, F32), "mm": sb(C, F32), "rg": sb(C, F32), "junk": sb(2 * C, BF), "junk2": sb(2 * C, BF),
-    "fla": sb(C, BF), "flb": sb(C, BF), "sca": sb(H, F16), "scb": sb(H, F16),
-    "bd": sb(24, F32), "sd": sb(24, F32), "rd": sb(48, F32), "xd": sb(48, F32), "yd": sb(48, F32), "ye": sb(24, F32),
-    "ae": sb(100, F32), "keep": sb(100, F32), "pp": sb(100, F32), "o2": sb(2, U16), "tab": sb(3 * 784, BF),
+    "sg": sb(C, F32), "mm": sb(C, F32), "cc": sb(2 * C, F32), "junk": sb(2 * C, BF), "junk2": sb(2 * C, BF),
+    "fla": sb(2 * C, BF), "flb": sb(2 * C, BF), "sca": sb(C, F16), "scb": sb(C, F16),
+    "bd": sb(24, F32), "sd": sb(24, F32), "rd": sb(48, F32), "xd": sb(48, F32), "ye": sb(24, F32),
+    "yd": sb(48, F32), "yl": sb(48, F32), "yh": sb(48, F32),
+    "ae": sb(100, F32), "keep": sb(100, F32), "pp": sb(100, F32), "o2": sb(6, U16), "tab": sb(TAB + 56, F32),
     "w1": sb(24, F32), "w2": sb(24, F32), "za": sb(24, F32), "h0": sb(96, F32), "h1": sb(96, F32), "hs": sb(96, F32),
-    "osl": sb(24, U16), "val": sb(C, BF), "win": sb(WIN, BF), "i16": sb(400, BF), "dk": sb(800, BF),
+    "osl": sb(24, U16), "val": sb(C, BF), "win": sb(WIN, BF), "dk": sb(800, BF),
     "sk": sb(SLOTS, F16), "mk": sb(24, F32), "ok": sb(24, U16),
-    "dd": sb(4 * C, BF), "dn": sb(3 * C, BF), "ff": sb(8 * C, BF), "i768": sb(2 * C, F32), "kr": sb(C, F32),
+    "dd": sb(4 * C, BF), "dn": sb(3 * C, BF), "ff": sb(8 * C, BF), "kr": sb(C, F32),
     "ya": sb(H, F32), "yb": sb(H, F32),
 }
 for _t in range(R + 1):
@@ -54,7 +57,7 @@ for _t in range(R):
 for _b in range(8):
     SCRATCH["ps%d" % _b] = ("psum", [128, 512], F32)
 
-POOL = {"v": 40, "a": 34, "p": 22, "g": 20, "d": 22}
+POOL = {"v": 40, "a": 34, "p": 22, "g": 22, "d": 20}
 SEMAPHORES = ["%s%d" % (k, i) for k in POOL for i in range(POOL[k])]
 SEMAPHORES += ["%s%d" % (k, t) for k in ("aq", "al", "sq", "sl") for t in range(R)]
 
@@ -151,11 +154,8 @@ def rank_program(g, core, T, topo):
     def scan(out, d0, d1, init, o0, o1, r, w):
         return add("v", lambda e: e.tensor_tensor_scan(out, d0, d1, init, o0, o1), r, w)
 
-    def red(out, in_, op, r, w):
-        return add("v", lambda e: e.tensor_reduce(out, in_, AxisListType.X, op), r, w)
-
-    def fill(ap, c, w):
-        return add("v", lambda e: e.memset(ap, c), "", w)
+    def fill(ap, c, w, r=""):
+        return add("v", lambda e: e.memset(ap, c), r, w)
 
     def quant(out, sc, in_, r, w):
         return add("v", lambda e: e.quantize_mx(out, sc, in_), r, w)
@@ -173,10 +173,10 @@ def rank_program(g, core, T, topo):
             return ts(out, in_, c, Op.mult, r, w)
         return act(out, in_, Fn.Copy, r, w, scale=c)
 
-    def iota(out, pat, base, cm, w, small=True):
+    def iota(out, pat, base, cm, w, small=True, r=""):
         if small:
-            return add("g", lambda e: e.iota(out, pat, base, cm, allow_small_or_imprecise_dtypes=True), "", w)
-        return add("g", lambda e: e.iota(out, pat, base, cm), "", w)
+            return add("g", lambda e: e.iota(out, pat, base, cm, allow_small_or_imprecise_dtypes=True), r, w)
+        return add("g", lambda e: e.iota(out, pat, base, cm), r, w)
 
     def mx(bank, n, lq, ls, rq, rs, start, stop, r):
         return add("p", lambda e: e.matmul_mx(T["ps%d" % bank][:, 0:n], lq, ls, rq, rs, start, stop), r, "ps%d" % bank)
@@ -194,9 +194,16 @@ def rank_program(g, core, T, topo):
     def arrival(src, name, writes, w):
         must.append(add("x", None, "", w, sem=(name, len(topo.engines(src, core)) * writes)))
 
-    names = ("pm pma pmb phi q4 q128 c1 low inv kap cf a32 th1a th1b th2a th2b u u2 th6 ts na nb beta gam f base").split()
+    names = ("pm pma pmb c1 phi low inv kap cf a32 q16 cb cg cq ce qu sl sh kq kp k2 k3 th1a th1b th2a th2b u cs bi ts na nb "
+             "s1 s2 f base").split()
     col = {n: T.col[:, i:i + 1] for i, n in enumerate(names)}
     u8 = dt.uint8
+    t1a, t1b, wm = T.tb[:, 0:33], T.tb[:, 40:73], T.tb[:, 80:113]
+    at = {k: 8 * (k - 3) for k in range(3, 8)}
+    th = {k: T.wn[:, at[k]:at[k] + 1] for k in at}
+
+    def line(out, a, b, w, r=""):
+        act(out, col["pm"], Fn.Identity, "pm " + r, w, bias=b, scale=a)
 
     dma("a", T.ut[:], T.u[:], "", "ut")
     dma("s", T.xt[:, 0:4 * H], T.x[:, 0:4 * H], "", "xta")
@@ -207,183 +214,209 @@ def rank_program(g, core, T, topo):
     dma("s", T.vt[:], T.v[:], "", "vt")
     iota(T.ip[:], [[0, 1]], 0, 1, "ip", small=False)
     iota(T.iu[:], [[1, 2], [16, 8]], 0, 0, "iu", small=False)
-    iota(T.i49[:], [[1, 49]], 0, 0, "i49")
+    iota(T.j16[:], [[1, 16]], 0, 0, "j16")
     fill(T.ep[:], 64.0, "ep")
-    fill(T.en[:], -64.0, "en")
     fill(T.c4[:], 4.0, "c4")
-    for n in ("ep", "en"):
-        if n == "en":
-            iota(T.i16[:], [[0, 25], [1, 16]], 0, 0, "i16")
-        add("g", lambda e, n=n: e.affine_select(T[n][:], T[n][:], [[1, 516]], Op.is_equal, 0.0, -3, -4), n, n)
     ts(T.ip2[:], T.ip[:], 15, Op.bitwise_and, "ip", "ip2")
+    fill(T.tb[:], 0.0, "tb")
     cp(T.ou[:], T.iu[:], "iu", "ou")
-    scan(T.g16[:], T.c4[:], T.c4[:], LO / 16, Op.mult, Op.mult, "c4", "g16")
     cp(col["pm"], T.ip2[:], "ip2", "pm")
+    scan(T.g16[:], T.c4[:], T.c4[:], LO / 16, Op.mult, Op.mult, "c4", "g16")
+    fill(T.h0[:], 1.0, "h0")
+    fill(T.ctab[:], 0.0, "ctab")
+    ts(T.oh[:], T.j16[:], col["pm"], Op.is_equal, "j16 pm", "oh")
+    line(col["pma"], 1.0, 1.0, "pma")
+    line(col["c1"], 0.5, 4.5, "c1")
+    line(col["pmb"], 1.0, 17.0, "pmb")
+    line(col["low"], LO * EPS / 4, LO * EPS / 4, "low")
+    line(T.tb[:, 33:34], LO * EPS / 128, LO * EPS / 128, "t1a3", "tb")
     joint("eighths")
-    fill(T.u0[:], 0.0, "u0")
+    fill(T.u0[:], 1.0, "u0")
     for k in range(4):
-        fill(T.c8[:, 1 + 8 * k:9 + 8 * k], 2.0 ** k / 8, "c8%d" % k)
-    for n in ("t1a", "t1b", "wm"):
-        fill(T[n][:, 0:1], 0.0, n + "0")
+        fill(T.t2[:, 1 + 8 * k:9 + 8 * k], 16.0 * 2 ** k, "t2%d" % k)
     joint(None)
-    ts(T.oh[:], T.i49[:, 0:16], col["pm"], Op.is_equal, "i49 pm", "oh")
-    ts(T.tri[:], T.i49[:, 0:16], col["pm"], Op.is_lt, "i49 pm", "tri")
-    ts(T.tmp[:, 16:17], col["pm"], -1.0, Op.mult, "pm", "tmpb", 4.0, Op.add)
-    ts(T.u0[:, 8:33:8], T.c8[:, 8:33:8], 8.0, Op.mult, "u0 c80 c81 c82 c83", "u8")
-    fill(T.u0[:, 33:34], 1.0 / 32, "u0")
-    tt(T.tmp[:, 0:16], T.g16[:, 1:17], T.oh[:], Op.mult, "g16 oh", "tmpa")
-    ts(T.off[:, 1:2], T.tmp[:, 16:17], 2.0, Op.max, "tmpb", "off1")
-    joint("cols")
-    for n, a, b in (("pma", 1.0, 1.0), ("pmb", 1.0, 17.0), ("q4", 0.25, 0.25), ("q128", 1.0 / 128, 1.0 / 128),
-                    ("c1", 0.125, 1.125), ("low", LO * EPS / 4, LO * EPS / 4), ("cf", -LO / 4096, LO * 127 / 4096),
-                    ("a32", 1.0 / 4096, 129.0 / 4096)):
-        act(col[n], col["pm"], Fn.Identity, "pm", n, bias=b, scale=a)
+    tt(T.tmp[:], T.g16[:, 1:17], T.oh[:], Op.mult, "g16 oh", "tmp")
+    joint("steps")
+    for k in at:
+        fill(T.ctab[:, at[k] + 2:at[k] + 3], 16.0 ** (7 - k), "step%d" % k, "ctab")
     joint(None)
-    red(col["th1a"], T.tmp[:, 0:16], Op.add, "tmpa", "th1a")
-    tt(col["phi"], col["c1"], col["q4"], Op.max, "c1 q4", "phi")
-    ts(T.t2[:, 1:33], T.u0[:, 1:33], col["q128"], Op.mult, "u0 u8 q128", "t2")
+    add("v", lambda e: e.tensor_reduce(col["th1a"], T.tmp[:], AxisListType.X, Op.add), "tmp", "th1a")
+    tt(col["phi"], col["pma"], col["c1"], Op.max, "pma c1", "phi")
+    quant(T.qu[:], T.su[:], T.ut[:], "ut", "qu")
     ts(col["th1b"], col["th1a"], 2.0 ** 64, Op.mult, "th1a", "th1b")
-    ts(T.t1a[:, 2:33], T.g16[:, 2:33], col["phi"], Op.mult, "g16 phi", "t1a2", EPS * 15 / 16, Op.mult)
-    ts(T.t1b[:, 1:33], T.g16[:, 1:33], col["phi"], Op.mult, "g16 phi", "t1b1", EPS * 15 / 4, Op.mult)
-    ts(T.t1a[:, 1:2], col["phi"], 16 * LO * EPS, Op.mult, "phi low", "t1a1", col["low"], Op.subtract)
-    tt(T.t2[:, 1:33], T.t2[:, 1:33], T.c8[:, 1:33], Op.add, "t2 c80 c81 c82 c83", "t2")
-    add("v", lambda e: e.reciprocal(col["inv"], col["phi"]), "phi", "inv")
-    act(T.t1a[:, 33:34], col["low"], Fn.Identity, "low", "t1a3", scale=1.0 / 32)
-    act(T.t1b[:, 33:34], col["phi"], Fn.Identity, "phi", "t1b3", scale=LO * EPS / 8)
-    act(col["kap"], col["phi"], Fn.Identity, "phi", "kap", scale=16 * LO)
-    act(T.ctab[:], T.i49[:, 0:40], Fn.Identity, "i49", "ctab0", scale=0.0)
-    steps = {3: 2.0 ** -7, 4: 2.0 ** -11, 5: 2.0 ** -15, 6: 2.0 ** -19, 7: 2.0 ** -23}
-    at = {k: 8 * ((k + 1) % 5) for k in steps}
-    cells = [(at[k] + 1, 0.0, steps[k]) for k in steps]
-    cells += [(at[k] + 3, steps[k + 1] - steps[k], steps[k + 1] - steps[k]) for k in (3, 4, 5)]
-    cells += [(at[6] + 3, steps[7] - steps[6], steps[7] / 2 - steps[6]), (at[7] + 3, -steps[7], -steps[7] / 2)]
-    joint("cells")
-    for c, a, b in cells:
-        act(T.ctab[:, c:c + 1], col["pm"], Fn.Identity, "pm ctab0", "ctab%d" % (c + 1), bias=b, scale=a)
-    joint(None)
-    ctab = " ".join("ctab%d" % (c + 1) for c, a, b in cells)
-    th = {k: T.wn[:, at[k] + 4:at[k] + 5] for k in steps}
+    ts(T.u0[:, 8:33:8], T.t2[:, 8:33:8], 2.0, Op.mult, "u0 t20 t21 t22 t23", "u8", 1.0, Op.add)
+    ts(T.off[:, 1:2], col["pm"], 3.0, Op.mult, "pm", "off1", 4.0, Op.min)
+    acopy(T.sp[:], T.su[:].indirect(T.ou[:]), "qu ou", "sp")
+    cp(T.qp[:].bitcast(dt.uint32), T.qu[:].bitcast(dt.uint32).indirect(T.ou[:]), "qu ou", "qp")
+    act(T.tb[:, 73:74], col["phi"], Fn.Identity, "phi tb", "t1b3", scale=LO * EPS / 32)
+    act(col["kap"], col["phi"], Fn.Identity, "phi", "kap", scale=4 * LO)
+    line(col["cf"], -LO / 4096, LO * 127 / 4096, "cf")
+    line(col["a32"], 1.0 / 32, 129.0 / 32, "a32")
+    line(col["q16"], 1.0 / 16, 17.0 / 16, "q16")
+    add("g", lambda e: e.affine_select(T.ep[:], T.ep[:], [[1, 516]], Op.is_equal, 0.0, -3, -4), "ep", "ep")
+    iota(T.h0[:, 0:96:4], [[0, 24]], 0, 0, "h0a", r="h0")
+    iota(T.h0[:, 1:96:4], [[1, 24]], DUMP, 24, "h0b", r="h0")
+    iota(T.tab[:], [[1, TAB + 56]], 0, 0, "tab")
 
-    def late_g():
-        iota(T.ae[:], [[0, 100]], 0, 0, "ae0")
-        iota(T.keep[:], [[0, 100]], 1, 0, "keep")
-        iota(T.keep[:, 50:51], [[0, 1]], 0, 0, "keep")
-        iota(T.tab[:, 0:784], [[0, 16], [1, 49]], 0, 0, "tab0")
-        iota(T.h0[:], [[0, 96]], 1, 0, "h0")
-        iota(T.h0[:, 0:96:4], [[0, 24]], 0, 0, "h0")
-        iota(T.h0[:, 1:96:4], [[1, 24]], DUMP, 24, "h0")
-        iota(T.val[:], [[1, 24], [24, 16]], -H, 0, "val")
-        iota(T.win[:, 0:SLOTS], [[0, SLOTS]], EMPTY, 0, "win")
+    def half(k, tile, h, r):
+        a = H * h
+        quant(T["qt%d" % k][:, a:a + H], T["st%d" % k][:, a:a + H], tile[:, 4 * a:4 * (a + H)], r, "qt%d%d" % (k, h))
 
-    def tri_a(lo, hi):
-        joint("tri")
-        for i in range(lo, hi):
-            act(T.tab[:, 784 + 49 * i:833 + 49 * i], T.i49[:], Fn.Identity, "i49 tri", "tab1_%d" % i, scale=T.tri[:, i:i + 1])
-        joint(None)
-    tab1 = " ".join("tab1_%d" % i for i in range(16))
+    def tables1():
+        add("v", lambda e: e.reciprocal(col["inv"], col["phi"]), "phi", "inv")
+        ts(T.tb[:, 2:33], T.g16[:, 2:33], col["phi"], Op.mult, "g16 phi tb", "t1a2", EPS * 15 / 64, Op.mult)
+        ts(T.tb[:, 41:73], T.g16[:, 1:33], col["phi"], Op.mult, "g16 phi tb", "t1b1", EPS * 15 / 16, Op.mult)
+
+    def tables2():
+        ts(T.tb[:, 1:2], col["phi"], 4 * LO * EPS, Op.mult, "phi low tb", "t1a1", col["low"], Op.subtract)
+        act(T.t2[:, 8:33:8], T.t2[:, 8:33:8], Fn.Identity, "t20 t21 t22 t23 q16 u8", "t2", scale=col["q16"])
+        act(T.wu[:], T.u0[:], Fn.Identity, "u8 inv", "wu", scale=col["inv"])
+
+    def ones():
+        fill(T.ae[:], 0.0, "ae0")
+        ts(T.keep[:], T.tab[:, 0:100], 50.0, Op.not_equal, "tab", "keep")
+
+    def shifts_v():
+        ts(T.ctab[:, 3:20:16], T.ctab[:, 2:19:16], col["pma"], Op.mult, "step3 step5 pma", "shift3", -15.0 / 16, Op.mult)
+        ts(T.ctab[:, 11:12], T.ctab[:, 10:11], col["pma"], Op.mult, "step4 pma", "shift", -15.0 / 256, Op.mult)
+        fill(T.win[:, 0:SLOTS], float(EMPTY), "win")
+
+    def shifts_a():
+        line(T.ctab[:, at[6] + 3:at[6] + 4], -15.0 / 16, -15.5 / 16, "shift6", "ctab")
+        line(T.ctab[:, at[7] + 3:at[7] + 4], -1.0 / 16, -0.5 / 16, "shift7", "ctab")
+    ctab = "step3 step4 step5 step6 step7 shift3 shift shift6 shift7"
 
     def qe(k):
-        src, b = ("ep", "en")[k // 4], min(k, 3)
-        quant(T.qe[:, 128 * k:128 * k + 128], T.se[:, 128 * k:128 * k + 128], T[src][:, 3 - b:515 - b], src, "qe%d" % k)
+        src = T.ep[:, 3 - k:515 - k] if k < 4 else T.en[:, 5 - k:517 - k]
+        quant(T.qe[:, 128 * k:128 * k + 128], T.se[:, 128 * k:128 * k + 128], src, ("ep", "en")[k // 4], "qe%d" % k)
 
-    def unpack(bank, k, qt, st, r, stop=True):
-        mx(bank, qt[1] - qt[0], T.qe[:, 128 * k:128 * k + 128], T.se[:, 128 * k:128 * k + 128],
-           T["%s" % st[0]][:, qt[0]:qt[1]], T["%s" % st[1]][:, qt[0]:qt[1]], True, stop, "qe%d %s" % (k, r))
+    def unpack(bank, k, a, b, pair, r, stop=True):
+        mx(bank, b - a, T.qe[:, 128 * k:128 * k + 128], T.se[:, 128 * k:128 * k + 128], pair[0][:, a:b], pair[1][:, a:b],
+           True, stop, "qe%d %s" % (k, r))
 
     def hold(out, c, w):
         ts(out, T.i16[:], col["pm"], Op.is_equal, "i16 pm", w, c, Op.mult)
 
-    def half(k, tile, h, r):
-        a = H * h
-        quant(T["qt%d" % k][:, a:a + H], T["st%d" % k][:, a:a + H], tile[:, 4 * a:4 * a + 4 * H], r, "qt%d%d" % (k, h))
+    def sums1():
+        line(col["cq"], 49.0, 24.0, "cq")
+        line(col["ce"], -49.0, 759.0, "ce")
+        line(col["kq"], 49.0, 784.0, "kq")
+        line(col["k2"], -49.0, -3088.0, "k2")
 
-    qe(0)
-    qe(1)
-    quant(T.qu[:], T.su[:], T.ut[:], "ut", "qu")
-    acopy(T.sp[:], T.su[:].indirect(T.ou[:]), "qu ou", "sp")
-    cp(T.qp[:].bitcast(dt.uint32), T.qu[:].bitcast(dt.uint32).indirect(T.ou[:]), "qu ou", "qp")
-    tri_a(0, 12)
-    half(0, T.xt, 0, "xta")
-    half(0, T.xt, 1, "xtb")
+    def sums2():
+        line(col["cb"], 49.0, -783.5, "cb")
+        line(col["cg"], -98.0, 1.0, "cg")
+        act(col["k3"], col["pm"], Fn.Identity, "pm k2", "k3", bias=11759.0, scale=col["k2"])
+        act(col["kp"], col["pm"], Fn.Identity, "pm kq", "kp", bias=392.0, scale=col["kq"])
 
-    def rest_a():
-        tri_a(12, 16)
-        dma("s", T.tab[:, 1568:2352], T.tab[:, 784:1568], tab1, "tab2")
-
-    def ends_a():
-        act(T.ae[:, 49:50], col["pm"], Fn.Identity, "pm ae0", "ae49", scale=49.0)
-        act(T.ae[:, 99:100], col["pm"], Fn.Identity, "pm ae0", "ae99", scale=49.0, bias=784.0)
-
-    idle_v = {(0, 2): lambda: (hold(T.dk[:, 0:800:2], HOLD, "dk0"), hold(T.dk[:, 1:800:2], 0.5, "dk1")),
-              (0, 3): lambda: (qe(2), qe(3), qe(4)),
-              (1, 3): lambda: quant(T.qv[:], T.sv[:], T.vt[:], "vt", "qv")}
-    idle_a = {(0, 2): rest_a, (0, 3): ends_a}
+    extra_v = {(0, 1): ones, (0, 2): shifts_v, (0, 3): lambda: (qe(0), qe(1), qe(2), qe(3)),
+               (1, 3): lambda: quant(T.qv[:], T.sv[:], T.vt[:], "vt", "qv")}
+    extra_a = {(0, 2): shifts_a, (0, 3): sums1, (0, 4): sums2}
 
     for t in range(R):
         mate = T.cores[rank ^ PARTNER[t]]
         qt, st, lq, ls, oa, la = (T["%s%d" % (n, t)] for n in ("qt", "st", "lq", "ls", "oa", "la"))
         tq = "qt%d0 qt%d1" % (t, t)
-        own, far = ("qt%d" % t, "st%d" % t), ("lq%d" % t, "ls%d" % t)
-        mx(0, H, T.qp[:, 128:256], T.sp[:, 128:256], qt[:, 0:H], st[:, 0:H], True, True, "qp sp qt%d0" % t)
-        mx(1, H, T.qp[:, 128:256], T.sp[:, 128:256], qt[:, H:C], st[:, H:C], True, True, "qp sp qt%d1" % t)
-        mx(2, C, T.qp[:, 0:128], T.sp[:, 0:128], qt[:], st[:], True, True, "qp sp " + tq)
+
+        def scores(h, rows):
+            a = H * h
+            for k in rows:
+                mx(2 - 2 * k + h, H, T.qp[:, 128 * k:128 * k + 128], T.sp[:, 128 * k:128 * k + 128], qt[:, a:a + H], st[:, a:a + H],
+                   True, True, "qp sp qt%d%d" % (t, h))
+
+        def size(h):
+            act(T.ab[:, H * h:H * h + H], T["ps%d" % (2 + h)][:, 0:H], Fn.Abs, "ps%d" % (2 + h), "ab%d" % h)
+
+        def base(h):
+            a = H * h
+            if t == 0:
+                ts(T.xx[:, a:a + H], T["ps%d" % h][:, 0:H], -1.0, Op.mult, "ps%d" % h, "x%d" % h, 0.0, Op.max)
+            else:
+                tt(T.xx[:, a:a + H], T.cc[:].indirect(T.ok[:, 12 * h:12 * h + 12]), T.nz[:, a:a + H], Op.add,
+                   "c0 c1 ok nz%d" % h, "x%d" % h)
+
+        def dear(h, out, w):
+            a = H * h
+            tt(out, T.xx[:, a:a + H], T.ab[:, a:a + H], Op.add, "x%d ab%d" % (h, h), w)
+
+        if t == 0:
+            half(0, T.xt, 0, "xta")
+            scores(0, (1, 0))
+            tables1()
+            size(0)
+            tables2()
+            half(0, T.xt, 1, "xtb")
+            scores(1, (0, 1))
+            base(0)
+            dear(0, T.xx[:, C:C + H], "x2")
+            size(1)
+            base(1)
+        else:
+            for h, k in ((0, 1), (1, 1), (0, 0), (1, 0)):
+                scores(h, (k,))
+            ts(T.nz[:, 0:H], T.ps0[:, 0:H], -1.0, Op.mult, "ps0", "nz0", 0.0, Op.max)
+            act(T.nz[:, H:C], T.ps1[:, 0:H], Fn.Relu, "ps1", "nz1", scale=-1.0)
+            size(0)
+            size(1)
+            base(0)
+            base(1)
+            dear(0, T.xx[:, C:C + H], "x2")
+        dear(1, T.ck[:], "ck")
         send([(lq[:].bitcast(u8), qt[:].bitcast(u8)), (ls[:], st[:])], mate, "aq%d" % t, "sq%d" % t, tq)
         arrival(mate, "aq%d" % t, 2, "lq%d" % t)
         if t == 0:
-            late_g()
-        if t == 1:
-            iota(T.i768[:], [[1, 2 * C]], 0, 0, "i768")
-        if t == 0:
-            for h in range(2):
-                ts(T.xx[:, H * h:H * h + H], T["ps%d" % h][:, 0:H], -1.0, Op.mult, "ps%d" % h, "x%d" % h, 0.0, Op.max)
-        else:
-            ts(T.nz[:, 0:H], T.ps0[:, 0:H], -1.0, Op.mult, "ps0", "nz0", 0.0, Op.max)
-            act(T.nz[:, H:C], T.ps1[:, 0:H], Fn.Relu, "ps1", "nz1", scale=-1.0)
-            for h in range(2):
-                a = H * h
-                tt(T.xx[:, a:a + H], T.mm[:, a:a + H], T.nz[:, a:a + H], Op.add, "mm nz%d" % h, "x%d" % h)
-        act(T.ab[:], T.ps2[:, 0:C], Fn.Abs, "ps2", "ab")
-        tt(T.xx[:, C:C + H], T.xx[:, 0:H], T.ab[:, 0:H], Op.add, "x0 ab", "x2")
-        tt(T.ck[:], T.xx[:, H:C], T.ab[:, H:C], Op.add, "x1 ab", "ck")
+            iota(T.i16[:], [[0, 25], [1, 16]], 0, 0, "i16")
+            iota(T.val[:], [[1, 24], [24, 16]], -H, 0, "val")
         dma("s", T.bd[:], T.xx[0:128:16, 0:C], "x0 x1", "bd")
 
-        def signs():
-            act(T.sg[:], T.ps2[:, 0:C], Fn.Copy, "ps2", "sg")
-            dma("s", T.sd[:], T.sg[0:128:16, :], "sg", "sd")
+        def parts(lo, hi):
+            return " ".join("x%d" % i for i in range(lo // H, (hi - 1) // H + 1 + (hi > C + H)))
+
+        def signs(h):
+            act(T.sg[:, H * h:H * h + H], T["ps%d" % (2 + h)][:, 0:H], Fn.Copy, "ps%d" % (2 + h), "sg%d" % h)
+            if h:
+                dma("s", T.sd[:], T.sg[0:128:16, :], "sg0 sg1", "sd")
+
+        def rest(h):
+            a = H + h * H // 2
+            tt(T.xx[:, C + a:C + a + H // 2], T.xx[:, a:a + H // 2], T.ab[:, a:a + H // 2], Op.add, "x1 ab1", "x%d" % (3 + h))
 
         def less(h):
-            a = C * h
-            ts(T.yy[:, a:a + C], T.xx[:, a:a + C], th[4], Op.subtract, "x%d x%d th4" % (2 * h, 2 * h + 1), "y%d" % h)
+            a, b = YY[h:h + 2]
+            ts(T.yy[:, a:b], T.xx[:, a:b], th[4], Op.subtract, parts(a, b) + " th4", "y%d" % h)
 
-        def spread():
+        def forks():
+            less(2)
             tt(T.xd[:, 0:48:2], T.bd[:], T.rd[:, 0:48:2], Op.add, "bd rd0", "xd0")
             tt(T.xd[:, 1:48:2], T.bd[:], T.rd[:, 1:48:2], Op.add, "bd rd1", "xd1")
             ts(T.ye[:], T.bd[:], th[4], Op.subtract, "bd th4", "ye")
+
+        def spread():
+            ts(T.yl[:], T.xd[:], th[4], Op.subtract, "xd0 xd1 th4 q", "yl", col["qu"], Op.add)
+            ts(T.yh[:], T.xd[:], th[4], Op.subtract, "xd0 xd1 th4 q", "yh", col["qu"], Op.subtract)
             ts(T.yd[:], T.xd[:], th[4], Op.subtract, "xd0 xd1 th4", "yd")
 
-        idle_a[t, 1] = signs
-        idle_a[t, 5] = lambda: (act(T.rd[:, 0:48:2], T.sd[:], Fn.Relu, "sd", "rd0", scale=-1.0),
-                                act(T.rd[:, 1:48:2], T.sd[:], Fn.Relu, "sd", "rd1"))
-        idle_v[t, 1] = lambda: tt(T.xx[:, C + H:2 * C], T.xx[:, H:C], T.ab[:, H:C], Op.add, "x1 ab", "x3")
-        idle_v[t, 4] = lambda: less(0)
-        idle_v[t, 5] = lambda: less(1)
-        idle_v[t, 6] = spread
+        every_a = {1: lambda: signs(0), 2: lambda: signs(1),
+                   5: lambda: (act(T.rd[:, 0:48:2], T.sd[:], Fn.Relu, "sd", "rd0", scale=-1.0),
+                               act(T.rd[:, 1:48:2], T.sd[:], Fn.Relu, "sd", "rd1"))}
+        every_v = {1: lambda: rest(0), 2: lambda: rest(1), 4: lambda: less(0), 5: lambda: less(1), 6: forks, 7: spread}
 
-        def quarters(name, lo, hi):
-            return " ".join("%s%d" % (name, i) for i in range(lo // H, (hi - 1) // H + 1))
+        def idle(every, extra, k):
+            every.get(k, lambda: 0)()
+            extra.get((t, k), lambda: 0)()
 
         def double(k, between, behind):
             both = list(zip("ba", ND[k][::-1], (T.junk2, T.junk), (T.flb, T.fla), (T.scb, T.sca)))
             for n, na, junk, fl, sc in both:
-                act(junk[:, 0:na], T.xx[:, 0:na], Fn.Sign, quarters("x", 0, na) + " th%d%s" % (k, n), "n%s junk%s" % (n, n),
+                act(junk[:, 0:na], T.xx[:, 0:na], Fn.Sign, parts(0, na) + " th%d%s" % (k, n), "n%s junk%s" % (n, n),
                     bias=col["th%d%s" % (k, n)], scale=-1.0, acc=col["n" + n])
-            idle_a.get((t, k), lambda: 0)()
+            idle(every_a, extra_a, k)
             for n, na, junk, fl, sc in both:
-                m, c = C + H - na, col["th%d%s" % (k, n)]
-                if m:
-                    ts(fl[:, 0:m], T.xx[:, na:C + H], c, Op.is_gt, quarters("x", na, C + H) + " th%d%s" % (k, n), "fl0" + n,
-                       2.0, Op.mult)
-                ts(fl[:, m:m + H], T.ck[:], c, Op.is_gt, "ck th%d%s" % (k, n), "fl1" + n, 2.0, Op.mult)
+                c = col["th%d%s" % (k, n)]
+                if na < C + H:
+                    ts(fl[:, H:2 * C - na], T.xx[:, na:C + H], c, Op.is_gt, parts(na, C + H) + " th%d%s" % (k, n),
+                       "fl0" + n, 2.0, Op.mult)
+                ts(fl[:, 0:H], T.ck[:], c, Op.is_gt, "ck th%d%s" % (k, n), "fl1" + n, 2.0, Op.mult)
             between()
             for n, na, junk, fl, sc in both:
                 nv = 2 * C - na
@@ -395,78 +428,88 @@ def rank_program(g, core, T, topo):
                 ts(T.ofd[:, i:i + 1], sc[:, nv // 2 - 1:nv // 2], col["n" + n], Op.is_gt, "sc%s n%s pm%s" % (n, n, n),
                    "ofd" + n, col["pm" + n], Op.mult)
 
-        def climb(out, table, bias, acc, r, w):
-            act(T[out][:], table[:, 0:33].indirect(T.ofd[:]), Fn.Identity, "ofda ofdb " + r, out + " " + w, bias=bias, acc=acc)
+        def climb(out, table, bias, scale, acc, r, w):
+            act(T[out][:, 0:32], table.indirect(T.ofd[:]), Fn.Identity, "ofda ofdb " + r, out + " " + w, bias=bias, scale=scale,
+                acc=acc)
 
-        def count(k, data, name, c, tc, between=None, behind=None):
-            na = NA[k]
-            n = H if name == "x" else C
-            toks = [" ".join("%s%d" % (name, i) for i in range(lo // n, (hi - 1) // n + 1)) for lo, hi in ((0, na), (na, 2 * C))]
-            act(T.junk[:, 0:na], data[:, 0:na], Fn.Sign, toks[0] + " " + tc, "na junka", bias=c, scale=-1.0, acc=col["na"])
-            idle_a.get((t, k), lambda: 0)()
-            nv = 2 * C - na
-            ts(T.fla[:, 0:nv], data[:, na:2 * C], c, Op.is_gt, toks[1] + " " + tc, "fl0a fl1a", 2.0, Op.mult)
-            if between:
-                between()
+        def count(k, between, behind=None):
+            na, nv, tc = NA[k], 2 * C - NA[k], " th%d" % k
+            data, mine, other = (T.xx, parts(0, na), parts(na, 2 * C)) if k < 7 else (T.yy, "y0 y1", "y1 y2")
+            act(T.junk[:, 0:na], data[:, 0:na], Fn.Sign, mine + tc, "na junka", bias=th[k], scale=-1.0, acc=col["na"])
+            idle(every_a, extra_a, k)
+            ts(T.fla[:, 0:nv], data[:, na:2 * C], th[k], Op.is_gt, other + tc, "fl0a fl1a", 2.0, Op.mult)
+            between()
             scan(T.sca[:, 0:nv // 2], T.fla[:, 0:nv // 2], T.fla[:, nv // 2:nv], -float(nv), Op.add, Op.add, "fl0a fl1a", "sca")
             if behind:
                 behind()
-            ts(T.off[:, 0:1], T.sca[:, nv // 2 - 1:nv // 2], col["na"], Op.is_gt, "sca na", "off0")
-
-        def step(k, out, r, w):
-            act(T.gat2[:], T.wn[:, at[k]:at[k] + 5].indirect(T.off[:]), Fn.Identity, "off0 off1 wn " + r, "gat2 " + w, acc=out)
-            idle_v.get((t, k), lambda: 0)()
+            ts(T.off[:, 0:1], T.sca[:, nv // 2 - 1:nv // 2], col["na"], Op.is_gt, "sca na", "off0", 1.0, Op.add)
 
         double(1, lambda: 0, lambda: 0)
-        climb("gat", T.t1b, T.t1b[:, 33:34], col["th2b"], "t1b0 t1b1 t1b3", "th2b")
-        climb("gat2", T.t1a, T.t1a[:, 33:34], col["th2a"], "t1a0 t1a1 t1a2 t1a3", "th2a")
-        idle_v[t, 1]()
-        double(2, lambda: (ts(T.lo[:, 0:1], col["th2b"], col["inv"], Op.mult, "th2b inv", "lo", 0.25, Op.mult),
+        climb("gat", t1b, T.tb[:, 73:74], 1.0, col["th2b"], "t1b1 t1b3", "th2b")
+        climb("gat2", t1a, T.tb[:, 33:34], 1.0, col["th2a"], "t1a1 t1a2 t1a3", "th2a")
+        idle(every_v, extra_v, 1)
+        double(2, lambda: (ts(T.lo[:, 0:1], col["th2b"], col["inv"], Op.mult, "th2b inv", "lo", 1.0 / 128, Op.mult),
                            ts(col["f"], col["th2b"], col["kap"], Op.is_lt, "th2b kap cf", "f", col["cf"], Op.mult)),
-               lambda: (ts(T.wm[:, 1:33], T.t2[:, 1:33], T.lo[:, 0:1], Op.mult, "lo t2", "wm1", LO / 4, Op.max),
-                        ts(col["base"], T.lo[:, 0:1], col["a32"], Op.mult, "lo a32 f", "base", col["f"], Op.subtract),
-                        ts(T.wu[:], T.u0[:], T.lo[:, 0:1], Op.mult, "lo u0 u8", "wu")))
-        climb("gat", T.wm, col["base"], th[3], "wm0 wm1 base", "th3")
-        climb("gat2", T.wu, T.wu[:, 33:34], col["u"], "wu", "u")
-        idle_v.get((t, 2), lambda: 0)()
-        count(3, T.xx, "x", th[3], "th3",
-              lambda: ts(col["u2"], col["u"], 2 * LO, Op.max, "u", "u2"),
-              lambda: ts(T.wn[:, 0:36], T.ctab[:, 0:36], col["u2"], Op.mult, "u2 ctab0 " + ctab, "wn th4 th5 w6 th7"))
-        step(3, th[4], "th3", "th4")
-        count(4, T.xx, "x", th[4], "th4")
-        step(4, th[5], "th4", "th5")
-        count(5, T.xx, "x", th[5], "th5")
-        step(5, col["th6"], "th5", "th6")
-        count(6, T.xx, "x", col["th6"], "th6", lambda: ts(th[6], col["th6"], th[4], Op.subtract, "th6 th4", "w6"))
-        step(6, th[7], "w6", "th7")
-        count(7, T.yy, "y", th[7], "th7")
-        step(7, col["ts"], "th7", "ts")
+               lambda: (ts(T.tb[:, 81:113], T.t2[:, 1:33], T.lo[:, 0:1], Op.mult, "lo t2 tb", "wm", LO / 4, Op.max),
+                        ts(col["base"], T.lo[:, 0:1], col["a32"], Op.mult, "lo a32 f", "base", col["f"], Op.subtract)))
+        climb("gat", wm, col["base"], 1.0, th[3], "wm base", "th3")
+        climb("gat2", T.wu[:], 0.0, col["th2b"], col["u"], "wu th2b", "u")
+        idle(every_v, extra_v, 2)
+        between = {3: lambda: ts(T.lo[:, 1:2], col["u"], 64 * LO, Op.max, "u", "ulp", 2.0 ** -28, Op.mult),
+                   4: lambda: ts(col["bi"], th[4], 1.0 / 16, Op.mult, "th4 wn", "bi", T.wn[:, 11:12], Op.add),
+                   5: lambda: ts(col["qu"], T.lo[:, 1:2], 0.25, Op.mult, "ulp", "q"),
+                   6: lambda: ts(col["cs"], th[6], th[4], Op.subtract, "th6 th4", "cs"),
+                   7: lambda: ts(col["bi"], th[7], 1.0 / 16, Op.mult, "th7 wn", "bi", T.wn[:, 35:36], Op.add)}
+        behind = {3: lambda: ts(T.wn[:, 1:40], T.ctab[:, 1:40], T.lo[:, 1:2], Op.mult, "ulp " + ctab, "wn th4 th5 th6 th7"),
+                  6: lambda: ts(col["bi"], col["cs"], 1.0 / 16, Op.mult, "cs wn", "bi", T.wn[:, 27:28], Op.add)}
+        for k in at:
+            count(k, between[k], behind.get(k))
+            out, w = (th[k + 1], "gat2 th%d" % (k + 1)) if k < 7 else (col["ts"], "gat2 ts")
+            if k in (3, 5):
+                act(T.gat2[:, 0:32], T.wn[:, at[k]:at[k] + 5].indirect(T.off[:]), Fn.Identity, "off0 off1 wn th%d" % k, w, acc=out)
+            else:
+                act(T.gat2[:, 0:16], T.wn[:, at[k]:at[k] + 3].indirect(T.off[:, 0:1]), Fn.Identity, "off0 wn bi th%d" % k, w,
+                    bias=col["bi"], acc=out)
+            idle(every_v, extra_v, k)
 
-        for b in range(4):
-            unpack(4 + b, b, (0, C), far, "lq%d" % t)
         for b in range(3):
-            unpack(b + b // 2, b, (0, C), own, tq)
+            unpack(b, b, H * (b // 2), C, (qt, st), tq)
+        for b in range(4):
+            unpack(4 + b, b, 0, C, (lq, ls), "lq%d" % t)
 
         ts(T.ae[:, 1:49], T.yd[:], col["ts"], Op.is_lt, "yd ts ae0", "aea")
         ts(T.ae[:, 51:99], T.yd[:], col["ts"], Op.is_equal, "yd ts ae0", "aee")
+        act(T.junk[:, 0:48], T.yl[:], Fn.Sign, "yl ts", "sl junka", bias=col["ts"], scale=-1.0, acc=col["sl"])
+        act(T.junk2[:, 0:48], T.yh[:], Fn.Sign, "yh ts", "sh junkb", bias=col["ts"], scale=-1.0, acc=col["sh"])
         act(T.w1[:], T.ye[:], Fn.Sign, "ye ts", "w1", bias=col["ts"], scale=-1.0)
         act(T.w2[:], T.w1[:], Fn.Identity, "w1", "w2", scale=-1024.0)
-        scan(T.pp[:], T.keep[:], T.ae[:], 0.0, Op.mult, Op.add, "keep aea aee ae49 ae99", "pp")
-        cp(T.o2[:], T.pp[:, 49:100:50], "pp", "o2")
-        act(T.gat2[:], T.tab[:, 0:1568].indirect(T.o2[:]), Fn.Identity, "o2 tab0 " + tab1, "gat2 beta",
-            bias=C / 32.0, scale=-1.0, acc=col["beta"])
-        act(T.gat[:], T.tab[:, 784:2352].indirect(T.o2[:]), Fn.Identity, "o2 tab2 " + tab1, "gat gam",
-            bias=-1.0 / 32, scale=2.0, acc=col["gam"])
+        ts(T.o2[:, 0:1], col["sl"], 0.5, Op.mult, "sl", "o0", TAB + 24.0, Op.add)
+        ts(T.o2[:, 1:2], col["sl"], -0.5, Op.mult, "sl ce", "o1", col["ce"], Op.add)
+        ts(T.o2[:, 4:5], col["sl"], 0.5, Op.mult, "sl cq", "o4", col["cq"], Op.add)
+        ts(T.o2[:, 2:3], col["sh"], 0.5, Op.mult, "sh ce", "o2", col["ce"], Op.add)
+        scan(T.pp[:], T.keep[:], T.ae[:], 0.0, Op.mult, Op.add, "keep aea aee", "pp")
+        if t == 0:
+            hold(T.dk[:, 0:800:2], HOLD, "dk0")
+        act(T.gat2[:], T.tab[:].indirect(T.o2[:, 0:3]), Fn.Relu, "o0 o1 o2 tab cb", "gat2 s1", bias=col["cb"], acc=col["s1"])
+        act(T.gat[:, 0:16], T.tab[:].indirect(T.o2[:, 4:5]), Fn.Relu, "o4 tab cg", "gat s2", bias=col["cg"], scale=2.0,
+            acc=col["s2"])
         tt(T.za[:], T.pp[:, 50:98:2], T.w2[:], Op.add, "pp w2", "za")
         tt(T.h1[:, 2:96:4], T.pp[:, 1:49:2], T.pp[:, 2:49:2], Op.add, "pp", "h1c")
-        ts(T.h1[:, 1:96:2], T.pp[:, 51:99], col["beta"], Op.min, "pp beta", "h1b")
-        ts(T.h1[:, 0:96:4], T.za[:], col["beta"], Op.is_ge, "za beta", "h1a")
+        ts(T.h1[:, 1:96:2], T.pp[:, 51:99], col["s1"], Op.add, "pp s1 kp", "h1b", col["kp"], Op.min)
+        ts(T.h1[:, 0:96:4], T.za[:], col["s1"], Op.add, "za s1 kp", "h1a", col["kp"], Op.is_ge)
+        act(T.rr[:, 0:2 * C:2], T.sg[:], Fn.Relu, "sg0 sg1", "r0", scale=-1.0)
+        act(T.rr[:, 1:2 * C:2], T.sg[:], Fn.Relu, "sg0 sg1", "r1")
+        for b in range(3):
+            a = H * (b // 2)
+            acopy(T.dn[:, C * b + a:C * b + C], T["ps%d" % b][:, 0:C - a], "ps%d" % b, "dn%d" % b)
         for b in range(4):
             act(T.dd[:, C * b:C * b + C], T["ps%d" % (4 + b)][:, 0:C], Fn.Copy, "ps%d" % (4 + b), "dd%d" % b, scale=1.0 / 64)
-        act(T.rr[:, 0:2 * C:2], T.sg[:], Fn.Relu, "sg", "r0", scale=-1.0)
-        act(T.rr[:, 1:2 * C:2], T.sg[:], Fn.Relu, "sg", "r1")
-        scan(T.hs[:], T.h0[:], T.h1[:], 0.0, Op.mult, Op.add, "h0 h1a h1b h1c", "hs")
-        ts(T.osl[:], T.hs[:, 3:96:4], col["gam"], Op.add, "hs gam", "osl")
+        if t == 0:
+            act(T.en[:], T.ep[:], Fn.Copy, "ep", "en", scale=-1.0)
+        scan(T.hs[:], T.h0[:], T.h1[:], 0.0, Op.mult, Op.add, "h0a h0b h1a h1b h1c", "hs")
+        if t == 0:
+            hold(T.dk[:, 1:800:2], 0.5, "dk1")
+        ts(T.osl[:], T.hs[:, 3:96:4], col["s2"], Op.subtract, "hs s2 k3", "osl", col["k3"], Op.add)
         cp(T.win[:].indirect(T.osl[:]), T.val[:], "osl val", "win")
         scan(T.sk[:], T.dk[:, 0:SLOTS], T.win[:, 0:SLOTS], 0.0, Op.add, Op.min, "dk0 dk1 win", "sk")
         tt(T.mk[:], T.sk[:, 31:2 * C:32], T.sk[:, 32:2 * C + 1:32], Op.min, "sk", "mk")
@@ -475,41 +518,41 @@ def rank_program(g, core, T, topo):
         arrival(mate, "al%d" % t, 1, "la%d" % t)
 
         ts(T.ok[:], T.mk[:], 2.0, Op.mult, "mk", "ok", float(C), Op.add)
-        acopy(T.rg[:], T.rr[:].indirect(T.ok[:]), "r0 r1 ok", "rg")
-        for b in range(3):
-            k = b + b // 2
-            acopy(T.dn[:, C * b:C * b + C], T["ps%d" % k][:, 0:C], "ps%d" % k, "dn%d" % b)
-        tt(T.mm[:], T.xx[:, 0:C].indirect(oa[:]), T.rg[:], Op.add, "x0 x1 oa%d rg" % t, "mm")
+        for s in range(2):
+            tt(T.cc[:, s:2 * C:2], T.xx[:, 0:C], T.rr[:, s:2 * C:2], Op.add, "x0 x1 r%d" % s, "c%d" % s)
+        if t == 0:
+            qe(4)
+            qe(5)
         if t < R - 1:
             iota(T.win[:, 0:SLOTS], [[0, SLOTS]], EMPTY, 0, "win")
         else:
-            must.append(dma("s", T.ml[:], T.mm[0:128:16, :], "mm", ""))
-            acopy(T.kr[:], T.i768[:].indirect(T.ok[:]), "i768 ok", "kr")
+            acopy(T.kr[:], T.tab[:].indirect(T.ok[:]), "tab ok", "kr")
             must.append(dma("s", T.kl[:], T.kr[0:128:16, :], "kr", ""))
-        for s in range(2):
-            unpack(6 + s, 3 + s, (0, H), own, "qt%d0" % t, False)
+        for b, s, h in ((2, 0, 0), (3, 0, 0), (2, 1, 0), (3, 1, 0), (3, 1, 1)):
+            unpack(BANK["%d%d%d" % (b, s, h)], b + 2 * s, H * h, H * h + H, (qt, st), tq, False)
 
         for call in TAIL:
             kind, q, h = call[:2], call[-1], int(call[-2])
             a, b = H * h, int(call[2])
             s = int(call[3]) if len(call) == 6 else 0
-            bank = 6 + s if b == 3 else 2 * b + h
+            laid = b - h > 1
+            bank = BANK.get("%d%d%d" % (b, s * laid, h))
             if kind == "zg":
                 (cp if q == "v" else acopy)(T.zt[:, 4 * a + b:4 * (a + H):4], T.dd[:, C * b:C * b + C].indirect(la[:, 12 * h:12 * h + 12]),
                                             "dd%d la%d" % (b, t), "zt%d%d" % (b, h))
             elif kind == "zq":
                 quant(T.qz[:, a:a + H], T.sz[:, a:a + H], T.zt[:, 4 * a:4 * (a + H)], " ".join("zt%d%d" % (i, h) for i in range(4)), "qz%d" % h)
             elif kind == "pd":
-                unpack(bank, 3 + s, (a, a + H), own, "qt%d%d" % (t, h), False)
+                unpack(bank, b + 2 * s, a, a + H, (qt, st), tq, False)
             elif kind == "pw":
                 mx(bank, H, T.qw[:, 128 * b:128 * b + 128], T.sw[:, 128 * b:128 * b + 128], T.qz[:, a:a + H], T.sz[:, a:a + H],
-                   b < 3, True, "qw sw qz%d" % h)
+                   not laid, True, "qw sw qz%d" % h)
             elif kind == "ev":
                 out, src = T.ff[:, 2 * C * b + 2 * a + s:2 * C * b + 2 * (a + H):2], T["ps%d" % bank][:, 0:H]
-                if b < 3:
-                    tt(out, T.dn[:, C * b + a:C * b + a + H], src, (Op.add, Op.subtract)[s], "ps%d dn%d" % (bank, b), "ff%d%d%d" % (b, s, h))
-                else:
+                if laid:
                     times(q, out, src, 1.0 - 2 * s, "ps%d" % bank, "ff%d%d%d" % (b, s, h))
+                else:
+                    tt(out, T.dn[:, C * b + a:C * b + a + H], src, (Op.add, Op.subtract)[s], "ps%d dn%d" % (bank, b), "ff%d%d%d" % (b, s, h))
             elif kind == "tg":
                 times(q, T.tt[:, 4 * a + b:4 * (a + H):4], T.ff[:, 2 * C * b:2 * C * (b + 1)].indirect(T.ok[:, 12 * h:12 * h + 12]),
                       1.0 / 64, "ff%d00 ff%d01 ff%d10 ff%d11 ok" % (b, b, b, b), "tt%d%d" % (b, h))
@@ -520,9 +563,11 @@ def rank_program(g, core, T, topo):
     for h in range(2):
         a = H * h
         mx(h, H, T.qv[:], T.sv[:], qt[:, a:a + H], st[:, a:a + H], True, True, "qv qt%d%d" % (R, h))
-        must.append(dma("s", T.oc[:, 4 * a:4 * a + 4 * H], qt[:, a:a + H].bitcast(u8), "qt%d%d" % (R, h), ""))
+        must.append(dma("s", T.oc[:, 4 * a:4 * (a + H)], qt[:, a:a + H].bitcast(u8), "qt%d%d" % (R, h), ""))
+    cp(T.mm[:], T.cc[:].indirect(T.ok[:]), "c0 c1 ok", "mm")
     acopy(T.ya[:], T.ps0[:, 0:H], "ps0", "ya")
     must.append(dma("a", T.y[:, 0:H], T.ya[:], "ya", ""))
+    must.append(dma("a", T.ml[:], T.mm[0:128:16, :], "mm", ""))
     cp(T.yb[:], T.ps1[:, 0:H], "ps1", "yb")
     for k in range(4):
         must.append(dma("sa"[k % 2], T.osc[4 * k:4 * k + 4, :], st[32 * k:32 * k + 4, :], tq, ""))

from concourse.mybir import dt, AluOpType, AxisListType, ActivationFunctionType

Op, Fn = AluOpType, ActivationFunctionType
C, R = 384, 3
H = C // 2
PARTNER = [1, 2, 1]
LO = 2.0 ** -59
EPS = 1 + 2.0 ** -15
NA = {3: 510, 4: 490, 5: 490, 6: 490, 7: 490}
ND = {1: (C + H, C), 2: (416, C)}
YY = (0, 320, 640, 2 * C)
EMPTY, HOLD = 512, 4096.0
SLOTS = 2 * C + 2
DUMP = 2 * C + 8
WIN = DUMP + 128 * 24 + 2 * C
TAB = 16 * 49
F32, BF, F16, U16, I32, Q, U8 = "float32", "bfloat16", "float16", "uint16", "int32", "float8_e4m3fn_x4", "uint8"
TAIL = ("zg30a zg10v zg20v zg00a zg11a zg31v zq0v pw100p pw210p zg01v zg21a zq1v pw000p ev100v ev110v pw310p pw300p "
        "ev210a pw001p ev010v pw200p ev000v ev310a ev001v pw311p pw101p ev011v ev111v ev300a pw201p ev101v pd301p pw301p "
        "ev200a ev211v ev311a ev201v tg01a tg00a ev301v tg11v tg10a tg30a tg20v tg21a tg31v tq0v tq1v").split()
BANK = {"000": 0, "201": 0, "100": 1, "101": 1, "001": 2, "311": 3, "200": 4, "210": 5, "300": 6, "301": 6, "310": 7}


def sb(n, d):
    return ("sbuf", [128, n], d)


SCRATCH = {
    "xt": sb(4 * C, BF), "tt": sb(4 * C, BF), "zt": sb(4 * C, BF), "ut": sb(512, BF), "vt": sb(512, BF),
    "qu": sb(128, Q), "su": sb(128, U8), "qp": sb(256, Q), "sp": sb(256, U8), "qv": sb(128, Q), "sv": sb(128, U8),
    "qw": sb(512, Q), "sw": sb(512, U8), "qz": sb(C, Q), "sz": sb(C, U8), "qe": sb(768, Q), "se": sb(768, U8),
    "ep": sb(516, BF), "en": sb(516, BF),
    "ip": sb(1, I32), "ip2": sb(1, I32), "iu": sb(16, I32), "ou": sb(16, U16), "i16": sb(400, BF), "j16": sb(16, F32),
    "col": sb(40, F32), "lo": sb(2, BF), "oh": sb(16, F32), "c4": sb(33, F32), "g16": sb(33, F32), "tmp": sb(16, F32),
    "tb": sb(120, F32), "t2": sb(33, F32), "u0": sb(33, F32), "wu": sb(33, F32),
    "ctab": sb(40, F32), "wn": sb(40, F32), "off": sb(2, U16), "ofd": sb(2, U16), "gat": sb(32, F32), "gat2": sb(48, F32),
    "xx": sb(2 * C, F32), "yy": sb(2 * C, F32), "rr": sb(2 * C, F32), "nz": sb(C, F32), "ab": sb(C, F32), "ck": sb(H, BF),
    "sg": sb(C, F32), "mm": sb(C, F32), "cc": sb(2 * C, F32), "junk": sb(2 * C, BF), "junk2": sb(2 * C, BF),
    "fla": sb(2 * C, BF), "flb": sb(2 * C, BF), "sca": sb(C, F16), "scb": sb(C, F16),
    "bd": sb(24, F32), "sd": sb(24, F32), "rd": sb(48, F32), "xd": sb(48, F32), "ye": sb(24, F32),
    "yd": sb(48, F32), "yl": sb(48, F32), "yh": sb(48, F32),
    "ae": sb(100, F32), "keep": sb(100, F32), "pp": sb(100, F32), "o2": sb(6, U16), "tab": sb(TAB + 56, F32),
    "w1": sb(24, F32), "w2": sb(24, F32), "za": sb(24, F32), "h0": sb(96, F32), "h1": sb(96, F32), "hs": sb(96, F32),
    "osl": sb(24, U16), "val": sb(C, BF), "win": sb(WIN, BF), "dk": sb(800, BF),
    "sk": sb(SLOTS, F16), "mk": sb(24, F32), "ok": sb(24, U16),
    "dd": sb(4 * C, BF), "dn": sb(3 * C, BF), "ff": sb(8 * C, BF), "kr": sb(C, F32),
    "ya": sb(H, F32), "yb": sb(H, F32),
}
for _t in range(R + 1):
    SCRATCH["qt%d" % _t] = sb(C, Q)
    SCRATCH["st%d" % _t] = sb(C, U8)
for _t in range(R):
    SCRATCH["lq%d" % _t] = sb(C, Q)
    SCRATCH["ls%d" % _t] = sb(C, U8)
    SCRATCH["oa%d" % _t] = sb(24, U16)
    SCRATCH["la%d" % _t] = sb(24, U16)
for _b in range(8):
    SCRATCH["ps%d" % _b] = ("psum", [128, 512], F32)

POOL = {"v": 40, "a": 34, "p": 22, "g": 22, "d": 20}
SEMAPHORES = ["%s%d" % (k, i) for k in POOL for i in range(POOL[k])]
SEMAPHORES += ["%s%d" % (k, t) for k in ("aq", "al", "sq", "sl") for t in range(R)]


def emit(g, T, ops):
    eng = {"v": g.vector, "a": g.scalar, "p": g.tensor, "g": g, "s": g.sync}
    writer, readers, known, after, waits, needed = {}, {}, {k: 0 for k in eng}, {}, [], set()
    group = {}
    for i, o in enumerate(ops):
        group.setdefault(o["grp"] or i, []).append(i)
    end = [group[o["grp"] or i][-1] for i, o in enumerate(ops)]
    for i, o in enumerate(ops):
        q = o["q"]
        deps = set(o["also"])
        for t in o["r"]:
            if t in writer:
                deps.add(writer[t])
            if t.startswith("ps"):
                deps.update(j for j in readers.get(t, []) if ops[j]["q"] != q)
        for t in o["w"]:
            if t in writer and not (q == "p" and ops[writer[t]]["q"] == "p"):
                deps.add(writer[t])
            deps.update(readers.get(t, []))
        mine = []
        deps = set(end[j] for j in deps)
        if q in eng:
            for j in sorted(deps, reverse=True):
                if not known[q] >> j & 1:
                    mine.append(j)
                    known[q] |= after[j]
            needed.update(mine)
            after[i] = known[q] | sum(1 << j for j in group[o["grp"] or i] if j <= i)
        else:
            after[i] = 1 << i
        waits.append((mine, known.get(q, 0)))
        for t in o["r"]:
            readers.setdefault(t, []).append(i)
        for t in o["w"]:
            writer[t] = i
            readers[t] = []
    last, count, mark, taken = {}, {}, {}, {}
    for i, o in enumerate(ops):
        q = o["q"]
        if o["sem"] is not None:
            mark[i] = o["sem"]
        if q not in eng:
            continue
        mine, kn = waits[i]
        for j in mine:
            eng[q].wait_ge(T.sem[mark[j][0]], mark[j][1])
        if o["f"] is None:
            continue
        ins = o["f"](eng[q])
        if o["sem"] is None and end[i] in needed:
            pool, step = ("d", 16) if o["dma"] else (q, 1)
            if end[i] not in taken:
                free = [n for n in ("%s%d" % (pool, k) for k in range(POOL[pool])) if n not in last or kn >> last[n] & 1]
                taken[end[i]] = free[0]
            name = taken[end[i]]
            last[name] = end[i]
            count[name] = count.get(name, 0) + step
            ins.then_inc(T.sem[name], step)
            mark[i] = (name, count[name])


def rank_program(g, core, T, topo):
    rank = T.rank_of(core)
    if rank is None:
        return
    ops, must, together = [], [], [None]

    def joint(name):
        together[0] = name

    def add(q, f, r, w, sem=None, dma=False, also=()):
        ops.append({"q": q, "f": f, "r": r.split(), "w": w.split(), "sem": sem, "dma": dma, "also": list(also),
                    "grp": together[0] and together[0] + q})
        return len(ops) - 1

    def dma(q, out, in_, r, w):
        return add(q, lambda e: e.dma_start(out, in_), r, w, dma=True)

    def ts(out, in0, s1, o0, r, w, s2=None, o1=None):
        if o1 is None:
            return add("v", lambda e: e.tensor_scalar(out, in0, s1, None, o0), r, w)
        return add("v", lambda e: e.tensor_scalar(out, in0, s1, s2, o0, o1), r, w)

    def tt(out, a, b, op, r, w):
        return add("v", lambda e: e.tensor_tensor(out, a, b, op), r, w)

    def cp(out, in_, r, w):
        return add("v", lambda e: e.tensor_copy(out, in_), r, w)

    def scan(out, d0, d1, init, o0, o1, r, w):
        return add("v", lambda e: e.tensor_tensor_scan(out, d0, d1, init, o0, o1), r, w)

    def fill(ap, c, w, r=""):
        return add("v", lambda e: e.memset(ap, c), r, w)

    def quant(out, sc, in_, r, w):
        return add("v", lambda e: e.quantize_mx(out, sc, in_), r, w)

    def act(out, in_, fn, r, w, bias=0.0, scale=1.0, acc=None):
        if acc is None:
            return add("a", lambda e: e.activation(out, in_, fn, bias=bias, scale=scale), r, w)
        return add("a", lambda e: e.activation(out, in_, fn, bias=bias, scale=scale, accum_out=acc), r, w)

    def acopy(out, in_, r, w):
        return add("a", lambda e: e.activation(out, in_, Fn.Copy), r, w)

    def times(q, out, in_, c, r, w):
        if q == "v":
            return ts(out, in_, c, Op.mult, r, w)
        return act(out, in_, Fn.Copy, r, w, scale=c)

    def iota(out, pat, base, cm, w, small=True, r=""):
        if small:
            return add("g", lambda e: e.iota(out, pat, base, cm, allow_small_or_imprecise_dtypes=True), r, w)
        return add("g", lambda e: e.iota(out, pat, base, cm), r, w)

    def mx(bank, n, lq, ls, rq, rs, start, stop, r):
        return add("p", lambda e: e.matmul_mx(T["ps%d" % bank][:, 0:n], lq, ls, rq, rs, start, stop), r, "ps%d" % bank)

    def send(pairs, dst, arrive, left, r):
        rid, pid = topo.addr(dst)[:2]
        mask = topo.mask(core, dst)
        n = len(topo.engines(core, dst)) * len(pairs)

        def f(e):
            for out, in_ in pairs:
                e.remote_dma(out, in_, T.sem[arrive], T.sem[left], pid, rid, mask)
        must.append(add("g", f, r, "", sem=(left, n)))

    def arrival(src, name, writes, w):
        must.append(add("x", None, "", w, sem=(name, len(topo.engines(src, core)) * writes)))

    names = ("pm pma pmb c1 phi low inv kap cf a32 q16 cb cg cq ce qu sl sh kq kp k2 k3 th1a th1b th2a th2b u cs bi ts na nb "
             "s1 s2 f base").split()
    col = {n: T.col[:, i:i + 1] for i, n in enumerate(names)}
    u8 = dt.uint8
    t1a, t1b, wm = T.tb[:, 0:33], T.tb[:, 40:73], T.tb[:, 80:113]
    at = {k: 8 * (k - 3) for k in range(3, 8)}
    th = {k: T.wn[:, at[k]:at[k] + 1] for k in at}

    def line(out, a, b, w, r=""):
        act(out, col["pm"], Fn.Identity, "pm " + r, w, bias=b, scale=a)

    dma("a", T.ut[:], T.u[:], "", "ut")
    dma("s", T.xt[:, 0:4 * H], T.x[:, 0:4 * H], "", "xta")
    dma("s", T.xt[:, 4 * H:4 * C], T.x[:, 4 * H:4 * C], "", "xtb")
    add("s", None, "xta xtb", "")
    dma("s", T.qw[:].bitcast(u8), T.wc[:], "", "qw")
    dma("s", T.sw[:], T.ws[:], "", "sw")
    dma("s", T.vt[:], T.v[:], "", "vt")
    iota(T.ip[:], [[0, 1]], 0, 1, "ip", small=False)
    iota(T.iu[:], [[1, 2], [16, 8]], 0, 0, "iu", small=False)
    iota(T.j16[:], [[1, 16]], 0, 0, "j16")
    fill(T.ep[:], 64.0, "ep")
    fill(T.c4[:], 4.0, "c4")
    ts(T.ip2[:], T.ip[:], 15, Op.bitwise_and, "ip", "ip2")
    fill(T.tb[:], 0.0, "tb")
    cp(T.ou[:], T.iu[:], "iu", "ou")
    cp(col["pm"], T.ip2[:], "ip2", "pm")
    scan(T.g16[:], T.c4[:], T.c4[:], LO / 16, Op.mult, Op.mult, "c4", "g16")
    fill(T.h0[:], 1.0, "h0")
    fill(T.ctab[:], 0.0, "ctab")
    ts(T.oh[:], T.j16[:], col["pm"], Op.is_equal, "j16 pm", "oh")
    line(col["pma"], 1.0, 1.0, "pma")
    line(col["c1"], 0.5, 4.5, "c1")
    line(col["pmb"], 1.0, 17.0, "pmb")
    line(col["low"], LO * EPS / 4, LO * EPS / 4, "low")
    line(T.tb[:, 33:34], LO * EPS / 128, LO * EPS / 128, "t1a3", "tb")
    joint("eighths")
    fill(T.u0[:], 1.0, "u0")
    for k in range(4):
        fill(T.t2[:, 1 + 8 * k:9 + 8 * k], 16.0 * 2 ** k, "t2%d" % k)
    joint(None)
    tt(T.tmp[:], T.g16[:, 1:17], T.oh[:], Op.mult, "g16 oh", "tmp")
    joint("steps")
    for k in at:
        fill(T.ctab[:, at[k] + 2:at[k] + 3], 16.0 ** (7 - k), "step%d" % k, "ctab")
    joint(None)
    add("v", lambda e: e.tensor_reduce(col["th1a"], T.tmp[:], AxisListType.X, Op.add), "tmp", "th1a")
    tt(col["phi"], col["pma"], col["c1"], Op.max, "pma c1", "phi")
    quant(T.qu[:], T.su[:], T.ut[:], "ut", "qu")
    ts(col["th1b"], col["th1a"], 2.0 ** 64, Op.mult, "th1a", "th1b")
    ts(T.u0[:, 8:33:8], T.t2[:, 8:33:8], 2.0, Op.mult, "u0 t20 t21 t22 t23", "u8", 1.0, Op.add)
    ts(T.off[:, 1:2], col["pm"], 3.0, Op.mult, "pm", "off1", 4.0, Op.min)
    acopy(T.sp[:], T.su[:].indirect(T.ou[:]), "qu ou", "sp")
    cp(T.qp[:].bitcast(dt.uint32), T.qu[:].bitcast(dt.uint32).indirect(T.ou[:]), "qu ou", "qp")
    act(T.tb[:, 73:74], col["phi"], Fn.Identity, "phi tb", "t1b3", scale=LO * EPS / 32)
    act(col["kap"], col["phi"], Fn.Identity, "phi", "kap", scale=4 * LO)
    line(col["cf"], -LO / 4096, LO * 127 / 4096, "cf")
    line(col["a32"], 1.0 / 32, 129.0 / 32, "a32")
    line(col["q16"], 1.0 / 16, 17.0 / 16, "q16")
    add("g", lambda e: e.affine_select(T.ep[:], T.ep[:], [[1, 516]], Op.is_equal, 0.0, -3, -4), "ep", "ep")
    iota(T.h0[:, 0:96:4], [[0, 24]], 0, 0, "h0a", r="h0")
    iota(T.h0[:, 1:96:4], [[1, 24]], DUMP, 24, "h0b", r="h0")
    iota(T.tab[:], [[1, TAB + 56]], 0, 0, "tab")

    def half(k, tile, h, r):
        a = H * h
        quant(T["qt%d" % k][:, a:a + H], T["st%d" % k][:, a:a + H], tile[:, 4 * a:4 * (a + H)], r, "qt%d%d" % (k, h))

    def tables1():
        add("v", lambda e: e.reciprocal(col["inv"], col["phi"]), "phi", "inv")
        ts(T.tb[:, 2:33], T.g16[:, 2:33], col["phi"], Op.mult, "g16 phi tb", "t1a2", EPS * 15 / 64, Op.mult)
        ts(T.tb[:, 41:73], T.g16[:, 1:33], col["phi"], Op.mult, "g16 phi tb", "t1b1", EPS * 15 / 16, Op.mult)

    def tables2():
        ts(T.tb[:, 1:2], col["phi"], 4 * LO * EPS, Op.mult, "phi low tb", "t1a1", col["low"], Op.subtract)
        act(T.t2[:, 8:33:8], T.t2[:, 8:33:8], Fn.Identity, "t20 t21 t22 t23 q16 u8", "t2", scale=col["q16"])
        act(T.wu[:], T.u0[:], Fn.Identity, "u8 inv", "wu", scale=col["inv"])

    def ones():
        fill(T.ae[:], 0.0, "ae0")
        ts(T.keep[:], T.tab[:, 0:100], 50.0, Op.not_equal, "tab", "keep")

    def shifts_v():
        ts(T.ctab[:, 3:20:16], T.ctab[:, 2:19:16], col["pma"], Op.mult, "step3 step5 pma", "shift3", -15.0 / 16, Op.mult)
        ts(T.ctab[:, 11:12], T.ctab[:, 10:11], col["pma"], Op.mult, "step4 pma", "shift", -15.0 / 256, Op.mult)
        fill(T.win[:, 0:SLOTS], float(EMPTY), "win")

    def shifts_a():
        line(T.ctab[:, at[6] + 3:at[6] + 4], -15.0 / 16, -15.5 / 16, "shift6", "ctab")
        line(T.ctab[:, at[7] + 3:at[7] + 4], -1.0 / 16, -0.5 / 16, "shift7", "ctab")
    ctab = "step3 step4 step5 step6 step7 shift3 shift shift6 shift7"

    def qe(k):
        src = T.ep[:, 3 - k:515 - k] if k < 4 else T.en[:, 5 - k:517 - k]
        quant(T.qe[:, 128 * k:128 * k + 128], T.se[:, 128 * k:128 * k + 128], src, ("ep", "en")[k // 4], "qe%d" % k)

    def unpack(bank, k, a, b, pair, r, stop=True):
        mx(bank, b - a, T.qe[:, 128 * k:128 * k + 128], T.se[:, 128 * k:128 * k + 128], pair[0][:, a:b], pair[1][:, a:b],
           True, stop, "qe%d %s" % (k, r))

    def hold(out, c, w):
        ts(out, T.i16[:], col["pm"], Op.is_equal, "i16 pm", w, c, Op.mult)

    def sums1():
        line(col["cq"], 49.0, 24.0, "cq")
        line(col["ce"], -49.0, 759.0, "ce")
        line(col["kq"], 49.0, 784.0, "kq")
        line(col["k2"], -49.0, -3088.0, "k2")

    def sums2():
        line(col["cb"], 49.0, -783.5, "cb")
        line(col["cg"], -98.0, 1.0, "cg")
        act(col["k3"], col["pm"], Fn.Identity, "pm k2", "k3", bias=11759.0, scale=col["k2"])
        act(col["kp"], col["pm"], Fn.Identity, "pm kq", "kp", bias=392.0, scale=col["kq"])

    extra_v = {(0, 1): ones, (0, 2): shifts_v, (0, 3): lambda: (qe(0), qe(1), qe(2), qe(3)),
               (1, 3): lambda: quant(T.qv[:], T.sv[:], T.vt[:], "vt", "qv")}
    extra_a = {(0, 2): shifts_a, (0, 3): sums1, (0, 4): sums2}

    for t in range(R):
        mate = T.cores[rank ^ PARTNER[t]]
        qt, st, lq, ls, oa, la = (T["%s%d" % (n, t)] for n in ("qt", "st", "lq", "ls", "oa", "la"))
        tq = "qt%d0 qt%d1" % (t, t)

        def scores(h, rows):
            a = H * h
            for k in rows:
                mx(2 - 2 * k + h, H, T.qp[:, 128 * k:128 * k + 128], T.sp[:, 128 * k:128 * k + 128], qt[:, a:a + H], st[:, a:a + H],
                   True, True, "qp sp qt%d%d" % (t, h))

        def size(h):
            act(T.ab[:, H * h:H * h + H], T["ps%d" % (2 + h)][:, 0:H], Fn.Abs, "ps%d" % (2 + h), "ab%d" % h)

        def base(h):
            a = H * h
            if t == 0:
                ts(T.xx[:, a:a + H], T["ps%d" % h][:, 0:H], -1.0, Op.mult, "ps%d" % h, "x%d" % h, 0.0, Op.max)
            else:
                tt(T.xx[:, a:a + H], T.cc[:].indirect(T.ok[:, 12 * h:12 * h + 12]), T.nz[:, a:a + H], Op.add,
                   "c0 c1 ok nz%d" % h, "x%d" % h)

        def dear(h, out, w):
            a = H * h
            tt(out, T.xx[:, a:a + H], T.ab[:, a:a + H], Op.add, "x%d ab%d" % (h, h), w)

        if t == 0:
            half(0, T.xt, 0, "xta")
            scores(0, (1, 0))
            tables1()
            size(0)
            tables2()
            half(0, T.xt, 1, "xtb")
            scores(1, (0, 1))
            base(0)
            dear(0, T.xx[:, C:C + H], "x2")
            size(1)
            base(1)
        else:
            for h, k in ((0, 1), (1, 1), (0, 0), (1, 0)):
                scores(h, (k,))
            ts(T.nz[:, 0:H], T.ps0[:, 0:H], -1.0, Op.mult, "ps0", "nz0", 0.0, Op.max)
            act(T.nz[:, H:C], T.ps1[:, 0:H], Fn.Relu, "ps1", "nz1", scale=-1.0)
            size(0)
            size(1)
            base(0)
            base(1)
            dear(0, T.xx[:, C:C + H], "x2")
        dear(1, T.ck[:], "ck")
        send([(lq[:].bitcast(u8), qt[:].bitcast(u8)), (ls[:], st[:])], mate, "aq%d" % t, "sq%d" % t, tq)
        arrival(mate, "aq%d" % t, 2, "lq%d" % t)
        if t == 0:
            iota(T.i16[:], [[0, 25], [1, 16]], 0, 0, "i16")
            iota(T.val[:], [[1, 24], [24, 16]], -H, 0, "val")
        dma("s", T.bd[:], T.xx[0:128:16, 0:C], "x0 x1", "bd")

        def parts(lo, hi):
            return " ".join("x%d" % i for i in range(lo // H, (hi - 1) // H + 1 + (hi > C + H)))

        def signs(h):
            act(T.sg[:, H * h:H * h + H], T["ps%d" % (2 + h)][:, 0:H], Fn.Copy, "ps%d" % (2 + h), "sg%d" % h)
            if h:
                dma("s", T.sd[:], T.sg[0:128:16, :], "sg0 sg1", "sd")

        def rest(h):
            a = H + h * H // 2
            tt(T.xx[:, C + a:C + a + H // 2], T.xx[:, a:a + H // 2], T.ab[:, a:a + H // 2], Op.add, "x1 ab1", "x%d" % (3 + h))

        def less(h):
            a, b = YY[h:h + 2]
            ts(T.yy[:, a:b], T.xx[:, a:b], th[4], Op.subtract, parts(a, b) + " th4", "y%d" % h)

        def forks():
            less(2)
            tt(T.xd[:, 0:48:2], T.bd[:], T.rd[:, 0:48:2], Op.add, "bd rd0", "xd0")
            tt(T.xd[:, 1:48:2], T.bd[:], T.rd[:, 1:48:2], Op.add, "bd rd1", "xd1")
            ts(T.ye[:], T.bd[:], th[4], Op.subtract, "bd th4", "ye")

        def spread():
            ts(T.yl[:], T.xd[:], th[4], Op.subtract, "xd0 xd1 th4 q", "yl", col["qu"], Op.add)
            ts(T.yh[:], T.xd[:], th[4], Op.subtract, "xd0 xd1 th4 q", "yh", col["qu"], Op.subtract)
            ts(T.yd[:], T.xd[:], th[4], Op.subtract, "xd0 xd1 th4", "yd")

        every_a = {1: lambda: signs(0), 2: lambda: signs(1),
                   5: lambda: (act(T.rd[:, 0:48:2], T.sd[:], Fn.Relu, "sd", "rd0", scale=-1.0),
                               act(T.rd[:, 1:48:2], T.sd[:], Fn.Relu, "sd", "rd1"))}
        every_v = {1: lambda: rest(0), 2: lambda: rest(1), 4: lambda: less(0), 5: lambda: less(1), 6: forks, 7: spread}

        def idle(every, extra, k):
            every.get(k, lambda: 0)()
            extra.get((t, k), lambda: 0)()

        def double(k, between, behind):
            both = list(zip("ba", ND[k][::-1], (T.junk2, T.junk), (T.flb, T.fla), (T.scb, T.sca)))
            for n, na, junk, fl, sc in both:
                act(junk[:, 0:na], T.xx[:, 0:na], Fn.Sign, parts(0, na) + " th%d%s" % (k, n), "n%s junk%s" % (n, n),
                    bias=col["th%d%s" % (k, n)], scale=-1.0, acc=col["n" + n])
            idle(every_a, extra_a, k)
            for n, na, junk, fl, sc in both:
                c = col["th%d%s" % (k, n)]
                if na < C + H:
                    ts(fl[:, H:2 * C - na], T.xx[:, na:C + H], c, Op.is_gt, parts(na, C + H) + " th%d%s" % (k, n),
                       "fl0" + n, 2.0, Op.mult)
                ts(fl[:, 0:H], T.ck[:], c, Op.is_gt, "ck th%d%s" % (k, n), "fl1" + n, 2.0, Op.mult)
            between()
            for n, na, junk, fl, sc in both:
                nv = 2 * C - na
                scan(sc[:, 0:nv // 2], fl[:, 0:nv // 2], fl[:, nv // 2:nv], -float(nv), Op.add, Op.add,
                     "fl0%s fl1%s" % (n, n), "sc" + n)
            behind()
            for n, na, junk, fl, sc in both:
                nv, i = 2 * C - na, "ab".index(n)
                ts(T.ofd[:, i:i + 1], sc[:, nv // 2 - 1:nv // 2], col["n" + n], Op.is_gt, "sc%s n%s pm%s" % (n, n, n),
                   "ofd" + n, col["pm" + n], Op.mult)

        def climb(out, table, bias, scale, acc, r, w):
            act(T[out][:, 0:32], table.indirect(T.ofd[:]), Fn.Identity, "ofda ofdb " + r, out + " " + w, bias=bias, scale=scale,
                acc=acc)

        def count(k, between, behind=None):
            na, nv, tc = NA[k], 2 * C - NA[k], " th%d" % k
            data, mine, other = (T.xx, parts(0, na), parts(na, 2 * C)) if k < 7 else (T.yy, "y0 y1", "y1 y2")
            act(T.junk[:, 0:na], data[:, 0:na], Fn.Sign, mine + tc, "na junka", bias=th[k], scale=-1.0, acc=col["na"])
            idle(every_a, extra_a, k)
            ts(T.fla[:, 0:nv], data[:, na:2 * C], th[k], Op.is_gt, other + tc, "fl0a fl1a", 2.0, Op.mult)
            between()
            scan(T.sca[:, 0:nv // 2], T.fla[:, 0:nv // 2], T.fla[:, nv // 2:nv], -float(nv), Op.add, Op.add, "fl0a fl1a", "sca")
            if behind:
                behind()
            ts(T.off[:, 0:1], T.sca[:, nv // 2 - 1:nv // 2], col["na"], Op.is_gt, "sca na", "off0", 1.0, Op.add)

        double(1, lambda: 0, lambda: 0)
        climb("gat", t1b, T.tb[:, 73:74], 1.0, col["th2b"], "t1b1 t1b3", "th2b")
        climb("gat2", t1a, T.tb[:, 33:34], 1.0, col["th2a"], "t1a1 t1a2 t1a3", "th2a")
        idle(every_v, extra_v, 1)
        double(2, lambda: (ts(T.lo[:, 0:1], col["th2b"], col["inv"], Op.mult, "th2b inv", "lo", 1.0 / 128, Op.mult),
                           ts(col["f"], col["th2b"], col["kap"], Op.is_lt, "th2b kap cf", "f", col["cf"], Op.mult)),
               lambda: (ts(T.tb[:, 81:113], T.t2[:, 1:33], T.lo[:, 0:1], Op.mult, "lo t2 tb", "wm", LO / 4, Op.max),
                        ts(col["base"], T.lo[:, 0:1], col["a32"], Op.mult, "lo a32 f", "base", col["f"], Op.subtract)))
        climb("gat", wm, col["base"], 1.0, th[3], "wm base", "th3")
        climb("gat2", T.wu[:], 0.0, col["th2b"], col["u"], "wu th2b", "u")
        idle(every_v, extra_v, 2)
        between = {3: lambda: ts(T.lo[:, 1:2], col["u"], 64 * LO, Op.max, "u", "ulp", 2.0 ** -28, Op.mult),
                   4: lambda: ts(col["bi"], th[4], 1.0 / 16, Op.mult, "th4 wn", "bi", T.wn[:, 11:12], Op.add),
                   5: lambda: ts(col["qu"], T.lo[:, 1:2], 0.25, Op.mult, "ulp", "q"),
                   6: lambda: ts(col["cs"], th[6], th[4], Op.subtract, "th6 th4", "cs"),
                   7: lambda: ts(col["bi"], th[7], 1.0 / 16, Op.mult, "th7 wn", "bi", T.wn[:, 35:36], Op.add)}
        behind = {3: lambda: ts(T.wn[:, 1:40], T.ctab[:, 1:40], T.lo[:, 1:2], Op.mult, "ulp " + ctab, "wn th4 th5 th6 th7"),
                  6: lambda: ts(col["bi"], col["cs"], 1.0 / 16, Op.mult, "cs wn", "bi", T.wn[:, 27:28], Op.add)}
        for k in at:
            count(k, between[k], behind.get(k))
            out, w = (th[k + 1], "gat2 th%d" % (k + 1)) if k < 7 else (col["ts"], "gat2 ts")
            if k in (3, 5):
                act(T.gat2[:, 0:32], T.wn[:, at[k]:at[k] + 5].indirect(T.off[:]), Fn.Identity, "off0 off1 wn th%d" % k, w, acc=out)
            else:
                act(T.gat2[:, 0:16], T.wn[:, at[k]:at[k] + 3].indirect(T.off[:, 0:1]), Fn.Identity, "off0 wn bi th%d" % k, w,
                    bias=col["bi"], acc=out)
            idle(every_v, extra_v, k)

        for b in range(3):
            unpack(b, b, H * (b // 2), C, (qt, st), tq)
        for b in range(4):
            unpack(4 + b, b, 0, C, (lq, ls), "lq%d" % t)

        ts(T.ae[:, 1:49], T.yd[:], col["ts"], Op.is_lt, "yd ts ae0", "aea")
        ts(T.ae[:, 51:99], T.yd[:], col["ts"], Op.is_equal, "yd ts ae0", "aee")
        act(T.junk[:, 0:48], T.yl[:], Fn.Sign, "yl ts", "sl junka", bias=col["ts"], scale=-1.0, acc=col["sl"])
        act(T.junk2[:, 0:48], T.yh[:], Fn.Sign, "yh ts", "sh junkb", bias=col["ts"], scale=-1.0, acc=col["sh"])
        act(T.w1[:], T.ye[:], Fn.Sign, "ye ts", "w1", bias=col["ts"], scale=-1.0)
        act(T.w2[:], T.w1[:], Fn.Identity, "w1", "w2", scale=-1024.0)
        ts(T.o2[:, 0:1], col["sl"], 0.5, Op.mult, "sl", "o0", TAB + 24.0, Op.add)
        ts(T.o2[:, 1:2], col["sl"], -0.5, Op.mult, "sl ce", "o1", col["ce"], Op.add)
        ts(T.o2[:, 4:5], col["sl"], 0.5, Op.mult, "sl cq", "o4", col["cq"], Op.add)
        ts(T.o2[:, 2:3], col["sh"], 0.5, Op.mult, "sh ce", "o2", col["ce"], Op.add)
        scan(T.pp[:], T.keep[:], T.ae[:], 0.0, Op.mult, Op.add, "keep aea aee", "pp")
        if t == 0:
            hold(T.dk[:, 0:800:2], HOLD, "dk0")
        act(T.gat2[:], T.tab[:].indirect(T.o2[:, 0:3]), Fn.Relu, "o0 o1 o2 tab cb", "gat2 s1", bias=col["cb"], acc=col["s1"])
        act(T.gat[:, 0:16], T.tab[:].indirect(T.o2[:, 4:5]), Fn.Relu, "o4 tab cg", "gat s2", bias=col["cg"], scale=2.0,
            acc=col["s2"])
        tt(T.za[:], T.pp[:, 50:98:2], T.w2[:], Op.add, "pp w2", "za")
        tt(T.h1[:, 2:96:4], T.pp[:, 1:49:2], T.pp[:, 2:49:2], Op.add, "pp", "h1c")
        ts(T.h1[:, 1:96:2], T.pp[:, 51:99], col["s1"], Op.add, "pp s1 kp", "h1b", col["kp"], Op.min)
        ts(T.h1[:, 0:96:4], T.za[:], col["s1"], Op.add, "za s1 kp", "h1a", col["kp"], Op.is_ge)
        act(T.rr[:, 0:2 * C:2], T.sg[:], Fn.Relu, "sg0 sg1", "r0", scale=-1.0)
        act(T.rr[:, 1:2 * C:2], T.sg[:], Fn.Relu, "sg0 sg1", "r1")
        for b in range(3):
            a = H * (b // 2)
            acopy(T.dn[:, C * b + a:C * b + C], T["ps%d" % b][:, 0:C - a], "ps%d" % b, "dn%d" % b)
        for b in range(4):
            act(T.dd[:, C * b:C * b + C], T["ps%d" % (4 + b)][:, 0:C], Fn.Copy, "ps%d" % (4 + b), "dd%d" % b, scale=1.0 / 64)
        if t == 0:
            act(T.en[:], T.ep[:], Fn.Copy, "ep", "en", scale=-1.0)
        scan(T.hs[:], T.h0[:], T.h1[:], 0.0, Op.mult, Op.add, "h0a h0b h1a h1b h1c", "hs")
        if t == 0:
            hold(T.dk[:, 1:800:2], 0.5, "dk1")
        ts(T.osl[:], T.hs[:, 3:96:4], col["s2"], Op.subtract, "hs s2 k3", "osl", col["k3"], Op.add)
        cp(T.win[:].indirect(T.osl[:]), T.val[:], "osl val", "win")
        scan(T.sk[:], T.dk[:, 0:SLOTS], T.win[:, 0:SLOTS], 0.0, Op.add, Op.min, "dk0 dk1 win", "sk")
        tt(T.mk[:], T.sk[:, 31:2 * C:32], T.sk[:, 32:2 * C + 1:32], Op.min, "sk", "mk")
        ts(oa[:], T.mk[:], H - 0.25, Op.add, "mk", "oa%d" % t)
        send([(la[:], oa[:])], mate, "al%d" % t, "sl%d" % t, "oa%d" % t)
        arrival(mate, "al%d" % t, 1, "la%d" % t)

        ts(T.ok[:], T.mk[:], 2.0, Op.mult, "mk", "ok", float(C), Op.add)
        for s in range(2):
            tt(T.cc[:, s:2 * C:2], T.xx[:, 0:C], T.rr[:, s:2 * C:2], Op.add, "x0 x1 r%d" % s, "c%d" % s)
        if t == 0:
            qe(4)
            qe(5)
        if t < R - 1:
            iota(T.win[:, 0:SLOTS], [[0, SLOTS]], EMPTY, 0, "win")
        else:
            acopy(T.kr[:], T.tab[:].indirect(T.ok[:]), "tab ok", "kr")
            must.append(dma("s", T.kl[:], T.kr[0:128:16, :], "kr", ""))
        for b, s, h in ((2, 0, 0), (3, 0, 0), (2, 1, 0), (3, 1, 0), (3, 1, 1)):
            unpack(BANK["%d%d%d" % (b, s, h)], b + 2 * s, H * h, H * h + H, (qt, st), tq, False)

        for call in TAIL:
            kind, q, h = call[:2], call[-1], int(call[-2])
            a, b = H * h, int(call[2])
            s = int(call[3]) if len(call) == 6 else 0
            laid = b - h > 1
            bank = BANK.get("%d%d%d" % (b, s * laid, h))
            if kind == "zg":
                (cp if q == "v" else acopy)(T.zt[:, 4 * a + b:4 * (a + H):4], T.dd[:, C * b:C * b + C].indirect(la[:, 12 * h:12 * h + 12]),
                                            "dd%d la%d" % (b, t), "zt%d%d" % (b, h))
            elif kind == "zq":
                quant(T.qz[:, a:a + H], T.sz[:, a:a + H], T.zt[:, 4 * a:4 * (a + H)], " ".join("zt%d%d" % (i, h) for i in range(4)), "qz%d" % h)
            elif kind == "pd":
                unpack(bank, b + 2 * s, a, a + H, (qt, st), tq, False)
            elif kind == "pw":
                mx(bank, H, T.qw[:, 128 * b:128 * b + 128], T.sw[:, 128 * b:128 * b + 128], T.qz[:, a:a + H], T.sz[:, a:a + H],
                   not laid, True, "qw sw qz%d" % h)
            elif kind == "ev":
                out, src = T.ff[:, 2 * C * b + 2 * a + s:2 * C * b + 2 * (a + H):2], T["ps%d" % bank][:, 0:H]
                if laid:
                    times(q, out, src, 1.0 - 2 * s, "ps%d" % bank, "ff%d%d%d" % (b, s, h))
                else:
                    tt(out, T.dn[:, C * b + a:C * b + a + H], src, (Op.add, Op.subtract)[s], "ps%d dn%d" % (bank, b), "ff%d%d%d" % (b, s, h))
            elif kind == "tg":
                times(q, T.tt[:, 4 * a + b:4 * (a + H):4], T.ff[:, 2 * C * b:2 * C * (b + 1)].indirect(T.ok[:, 12 * h:12 * h + 12]),
                      1.0 / 64, "ff%d00 ff%d01 ff%d10 ff%d11 ok" % (b, b, b, b), "tt%d%d" % (b, h))
            else:
                half(t + 1, T.tt, h, " ".join("tt%d%d" % (i, h) for i in range(4)))

    qt, st, tq = T["qt%d" % R], T["st%d" % R], "qt%d0 qt%d1" % (R, R)
    for h in range(2):
        a = H * h
        mx(h, H, T.qv[:], T.sv[:], qt[:, a:a + H], st[:, a:a + H], True, True, "qv qt%d%d" % (R, h))
        must.append(dma("s", T.oc[:, 4 * a:4 * (a + H)], qt[:, a:a + H].bitcast(u8), "qt%d%d" % (R, h), ""))
    cp(T.mm[:], T.cc[:].indirect(T.ok[:]), "c0 c1 ok", "mm")
    acopy(T.ya[:], T.ps0[:, 0:H], "ps0", "ya")
    must.append(dma("a", T.y[:, 0:H], T.ya[:], "ya", ""))
    must.append(dma("a", T.ml[:], T.mm[0:128:16, :], "mm", ""))
    cp(T.yb[:], T.ps1[:, 0:H], "ps1", "yb")
    for k in range(4):
        must.append(dma("sa"[k % 2], T.osc[4 * k:4 * k + 4, :], st[32 * k:32 * k + 4, :], tq, ""))
    must.append(dma("s", T.y[:, H:C], T.yb[:], "yb", ""))
    add("g", None, "", "", also=must)
    emit(g, T, ops)
